import numpy as np
import ml_dtypes


def mxq(x, axis, fmt="e4m3"):
    dtype, down = {"e4m3": (ml_dtypes.float8_e4m3fn, 7), "e5m2": (ml_dtypes.float8_e5m2, 14)}[fmt]
    v = np.moveaxis(np.asarray(x, np.float32).astype(ml_dtypes.bfloat16).astype(np.float64), axis, -1)
    blocks = v.reshape(v.shape[:-1] + (-1, 32))
    amax = np.abs(blocks).max(-1, keepdims=True)
    byte = np.maximum(np.where(amax > 0, np.frexp(amax)[1] - 1 + 127, 0) - down, 1)
    scale = np.exp2(byte - 127.0)
    codes = (blocks / scale).astype(np.float32).astype(dtype).astype(np.float64)
    return np.moveaxis((codes * scale).reshape(v.shape), -1, axis)


WIDE = False


def mx_kscale(k):
    if not WIDE:
        return np.ones(k)
    levels = np.array([10, -10, 5, -5, 0])
    if k % 512:
        return np.exp2(np.random.permutation(np.resize(levels, k // 32))).repeat(32)
    a = np.empty((k // 512, 16))
    for p in range(k // 512):
        a[p, :8] = np.random.permutation(np.resize(levels, 8))
        for g in range(8):
            far = levels[np.abs(levels - a[p, g]) >= 10]
            a[p, g + 8] = far[np.random.randint(len(far))]
    return np.exp2(a.ravel()).repeat(32)


BF16 = ml_dtypes.bfloat16


def bf(x):
    return np.asarray(x, np.float32).astype(BF16)


def f64(x):
    return np.asarray(x).astype(np.float64)


N, F, S, B = 2048, 1024, 1024, 1024

CAP = 2.0


def draw0():
    s = mx_kscale(F)
    t = mx_kscale(N)
    sens = np.random.standard_normal((N, F)) / np.sqrt(F)
    shocks = np.random.standard_normal((F, S))
    tilt = 0.5 * np.random.standard_normal(N)
    cap = CAP * (1 + 0.1 * np.random.standard_normal(N))
    short = np.random.standard_normal((B, N)) / np.sqrt(N)
    return {"sens": bf(sens * s * t[:, None]),
            "shocks": bf(shocks / s[:, None]),
            "tilt": bf(tilt * t),
            "cap": bf(cap * t * t),
            "short": bf(short / (t * t))}


def core(sens, shocks, tilt, cap, short):
    y = mxq(f64(sens), 1, "e4m3") @ mxq(f64(shocks), 0, "e4m3")
    v = y * (y + f64(tilt)[:, None])
    v = np.minimum(v, f64(cap)[:, None])
    loss = mxq(f64(short), 1, "e4m3") @ mxq(v, 0, "e4m3")
    return loss


def e4m3fn_bytes(y):
    return np.clip(np.asarray(y, np.float64), -448.0, 448.0).astype(np.float32).astype(ml_dtypes.float8_e4m3fn).view(np.uint8)


def e4m3fn_values(b):
    return np.asarray(b, np.uint8).view(ml_dtypes.float8_e4m3fn).astype(np.float64)


def setup_inputs():
    d = draw0()
    x0 = np.asarray(d['short']).astype(np.float64)
    s = (np.max(np.abs(x0), axis=(0,), keepdims=True) / 448.0).astype(np.float32)
    out = {}
    for k, v in d.items():
        if k == 'short':
            out['short_bytes'] = e4m3fn_bytes(x0 / s.astype(np.float64))
            out['short_scale'] = s
        else:
            out[k] = v
    return out


def reference(sens, shocks, tilt, cap, short_bytes, short_scale):
    return core(sens, shocks, tilt, cap, e4m3fn_values(short_bytes) * short_scale.astype(np.float64))

@@ -1,0 +1,385 @@
+from contextlib import ExitStack
+
+import concourse.mybir as mybir
+from concourse.masks import make_identity
+
+N, F, S, B = 2048, 1024, 1024, 1024
+FLOPS = 2 * N * F * S + 2 * B * N * S
+
+F32 = mybir.dt.float32
+BF16 = mybir.dt.bfloat16
+U32 = mybir.dt.uint32
+U8 = mybir.dt.uint8
+FP8 = mybir.dt.float8_e4m3fn
+FP8X4 = mybir.dt.float8_e4m3fn_x4
+ALU = mybir.AluOpType
+ACT = mybir.ActivationFunctionType
+
+P = 128
+PACK = 4
+K_PASS = P * PACK
+F_PASSES = F // K_PASS
+GROUPS = N // K_PASS
+HALF = S // 2
+BOOK_TILES = B // P
+
+SHOCKS_SHARE = 384
+V_SHARE = {(1, 1): 0, (2, 0): 384, (2, 1): 384, (3, 0): 384, (3, 1): 0}
+
+WIDE_GROUPS = (1, 2)
+
+ORDERED_TILES = (5, 6, 7)
+
+
+def tile_scenario_delta_gamma_losses_s7_kernel(
+    tc, sens, shocks, tilt, cap, short_bytes, short_scale, out
+):
+    nc = tc.nc
+    with ExitStack() as ctx:
+        keep = ctx.enter_context(tc.tile_pool(name="keep", bufs=1))
+        work = ctx.enter_context(tc.tile_pool(name="work", bufs=2))
+        psum = ctx.enter_context(tc.psum_pool(name="psum", bufs=8))
+
+        warm = keep.tile([P, 1], F32, name="warm")
+        nc.vector.memset(warm[:], 0.0)
+        nc.scalar.activation(out=warm[:], in_=warm[:], func=ACT.Square)
+        ident = keep.tile([P, P], F32, name="ident")
+        make_identity(nc, ident[:])
+
+        tilt_raw = keep.tile([P, GROUPS, 16], BF16, name="tilt_raw")
+        cap_raw = keep.tile([P, GROUPS, 16], BF16, name="cap_raw")
+        nc.scalar.dma_start(out=tilt_raw[:, :, 0:PACK], in_=tilt.rearrange("(g m t) -> m g t", m=P, t=PACK))
+        nc.scalar.dma_start(out=cap_raw[:, :, 0:PACK], in_=cap.rearrange("(g m t) -> m g t", m=P, t=PACK))
+        half_tilt = keep.tile([P, GROUPS, PACK], F32, name="half_tilt")
+        half_tilt_sq = keep.tile([P, GROUPS, PACK], F32, name="half_tilt_sq")
+        cap_f32 = keep.tile([P, GROUPS, PACK], F32, name="cap_f32")
+
+        def row_constants():
+            nc.vector.tensor_scalar(
+                out=half_tilt[:], in0=tilt_raw[:, :, 0:PACK], scalar1=0.5, scalar2=None, op0=ALU.mult
+            )
+            nc.vector.tensor_copy(out=cap_f32[:], in_=cap_raw[:, :, 0:PACK])
+            nc.vector.tensor_tensor(out=half_tilt_sq[:], in0=half_tilt[:], in1=half_tilt[:], op=ALU.mult)
+
+        sens_view = sens.rearrange("(g m t) k -> g m t k", m=P, t=PACK)
+        shocks_view = shocks.rearrange("(g p t) s -> g p t s", p=P, t=PACK)
+        bytes_view = short_bytes.rearrange("(i p) k -> p i k", p=P)
+        sens_rows = {}
+        shocks_raw = {}
+        bytes_sb = keep.tile([P, BOOK_TILES, N], U8, name="bytes_sb")
+        scale_sb = keep.tile([P, N], F32, name="scale_sb")
+
+        def load_sens(g, t0, n):
+            rows = keep.tile([P, n, F], BF16, name="sens_rows_%d_%d" % (g, t0))
+            nc.sync.dma_start(out=rows[:], in_=sens_view[g][:, t0 : t0 + n, :])
+            for t in range(n):
+                sens_rows[(g, t0 + t)] = rows[:, t, :]
+
+        def load_shocks(g, h):
+            raw = keep.tile([P, PACK, HALF], BF16, name="shocks_raw_%d_%d" % (g, h))
+            nc.sync.dma_start(out=raw[:], in_=shocks_view[g][:, :, h * HALF : (h + 1) * HALF])
+            shocks_raw[(g, h)] = raw
+
+        def load_bytes(i0, i1):
+            nc.sync.dma_start(out=bytes_sb[:, i0:i1, :], in_=bytes_view[:, i0:i1, :])
+
+        load_shocks(0, 0)
+        load_sens(0, 0, 2)
+        load_shocks(1, 0)
+        load_sens(0, 2, 2)
+        load_shocks(0, 1)
+        load_shocks(1, 1)
+        load_sens(1, 0, 4)
+        load_sens(2, 0, 4)
+        nc.sync.dma_start(out=scale_sb[:], in_=short_scale.rearrange("o k -> (o k)").partition_broadcast(P))
+        load_bytes(0, 2)
+        load_sens(3, 0, 4)
+        load_bytes(2, 5)
+        load_bytes(5, 8)
+
+        ctx.enter_context(tc.manual_schedule())
+
+        shocks_codes = keep.tile([P, F_PASSES, S], U32, name="shocks_codes", align_bytes=64)
+        shocks_scales = keep.tile([P, F_PASSES, S], U8, name="shocks_scales", align_bytes=64)
+        v_codes = [keep.tile([P, S], U32, name="v_codes_%d" % g, align_bytes=64) for g in range(GROUPS)]
+        v_scales = [keep.tile([P, S], U8, name="v_scales_%d" % g, align_bytes=64) for g in range(GROUPS)]
+
+        def half_cols(h):
+            return slice(h * HALF, (h + 1) * HALF)
+
+        def interleave(dst, src, vector_cols):
+            d = dst.rearrange("p (b c) t -> p b t c", c=4)
+            s = src.rearrange("p t (b c) -> p b t c", c=4)
+            cut = vector_cols // 4
+            if cut > 0:
+                nc.vector.tensor_copy(out=d[:, 0:cut], in_=s[:, 0:cut])
+            if cut < HALF // 4:
+                nc.scalar.copy(out=d[:, cut:], in_=s[:, cut:])
+
+        shocks_grouped = {}
+
+        def shocks_interleave(g, h):
+            shocks_grouped[(g, h)] = work.tile([P, HALF, PACK], BF16, name="shocks_grouped", align_bytes=64)
+            interleave(shocks_grouped[(g, h)][:], shocks_raw[(g, h)][:], SHOCKS_SHARE)
+
+        def shocks_quantise(g, h):
+            nc.vector.quantize_mx(
+                out=shocks_codes[:, g, half_cols(h)].bitcast(FP8X4),
+                scales=shocks_scales[:, g, half_cols(h)],
+                in_=shocks_grouped[(g, h)][:].rearrange("p n t -> p (n t)"),
+            )
+
+        def copy_words_out(dst, bank):
+            words = dst.rearrange("p q m j -> p (q m j)").bitcast(F32)
+            nc.scalar.copy(
+                out=words.rearrange("p (q m u) -> p q m u", q=2, u=2),
+                in_=bank.rearrange("p q u m -> p q m u"),
+            )
+
+        sens_bank = {}
+        sens_grouped = {}
+        sens_operand = {}
+
+        def sens_transpose(g, t):
+            sens_bank[(g, t)] = psum.tile([P, F_PASSES, 2, P], F32, name="bank")
+            words = sens_rows[(g, t)].bitcast(F32)
+            for q in range(F_PASSES):
+                for u in range(2):
+                    nc.tensor.transpose(
+                        sens_bank[(g, t)][:, q, u, :], words[:, 256 * q + u : 256 * (q + 1) : 2], ident[:]
+                    )
+
+        def sens_copy(g, t):
+            if t % 2 == 0:
+                sens_grouped[(g, t // 2)] = work.tile(
+                    [P, 2, F_PASSES, P, PACK], BF16, name="sens_grouped", align_bytes=64
+                )
+            copy_words_out(sens_grouped[(g, t // 2)][:, t % 2], sens_bank[(g, t)][:])
+
+        def sens_quantise(g, pair):
+            codes = work.tile([P, 2, F_PASSES, P], U32, name="sens_codes", align_bytes=64, bufs=5)
+            scales = work.tile([P, 2, F_PASSES, P], U8, name="sens_scales", align_bytes=64, bufs=5)
+            nc.vector.quantize_mx(
+                out=codes[:].rearrange("p a q m -> p (a q m)").bitcast(FP8X4),
+                scales=scales[:].rearrange("p a q m -> p (a q m)"),
+                in_=sens_grouped[(g, pair)][:].rearrange("p a q m j -> p (a q m j)"),
+            )
+            sens_operand[(g, pair)] = (codes, scales)
+
+        y_bank = {}
+        squares = {}
+        v_rows = {}
+        v_grouped = {}
+
+        def y_product(g, t, h):
+            codes, scales = sens_operand[(g, t // 2)]
+            y_bank[(g, t, h)] = psum.tile([P, HALF], F32, name="bank")
+            for q in range(F_PASSES):
+                nc.tensor.matmul_mx(
+                    out=y_bank[(g, t, h)][:],
+                    lhsT=codes[:, t % 2, q, :].bitcast(FP8X4),
+                    lhsT_scale=scales[:, t % 2, q, :],
+                    rhs=shocks_codes[:, q, half_cols(h)].bitcast(FP8X4),
+                    rhs_scale=shocks_scales[:, q, half_cols(h)],
+                    start=(q == 0),
+                    stop=(q == F_PASSES - 1),
+                )
+
+        def y_square(g, t, h):
+            if (g, t) not in squares:
+                squares[(g, t)] = work.tile([P, S], F32, name="squares", bufs=5)
+            nc.scalar.activation(
+                out=squares[(g, t)][:, half_cols(h)],
+                in_=y_bank[(g, t, h)][:],
+                func=ACT.Square,
+                bias=half_tilt[:, g, t : t + 1],
+            )
+
+        def v_clip(g, t, cols):
+            if g not in v_rows:
+                v_rows[g] = work.tile([P, PACK, S], BF16, name="v_rows")
+            nc.vector.tensor_scalar(
+                out=v_rows[g][:, t, cols],
+                in0=squares[(g, t)][:, cols],
+                scalar1=half_tilt_sq[:, g, t : t + 1],
+                scalar2=cap_f32[:, g, t : t + 1],
+                op0=ALU.subtract,
+                op1=ALU.min,
+            )
+
+        def v_interleave(g, h):
+            v_grouped[(g, h)] = work.tile([P, HALF, PACK], BF16, name="v_grouped", align_bytes=64, bufs=3)
+            interleave(v_grouped[(g, h)][:], v_rows[g][:, :, half_cols(h)], V_SHARE.get((g, h), HALF))
+
+        def v_quantise(g, h):
+            nc.vector.quantize_mx(
+                out=v_codes[g][:, half_cols(h)].bitcast(FP8X4),
+                scales=v_scales[g][:, half_cols(h)],
+                in_=v_grouped[(g, h)][:].rearrange("p n t -> p (n t)"),
+            )
+
+        short_wide = {}
+        short_words = {}
+        short_bank = {}
+        short_grouped = {}
+        short_operand = {}
+
+        def short_widen(i):
+            short_wide[i] = work.tile([P, N], BF16, name="short_wide", bufs=3)
+            nc.vector.tensor_tensor(
+                out=short_wide[i][:], in0=bytes_sb[:, i, :].bitcast(FP8), in1=scale_sb[:], op=ALU.mult
+            )
+
+        def short_order(i):
+            short_words[i] = work.tile([P, GROUPS, 2, P], F32, name="short_words")
+            words = short_wide[i][:].bitcast(F32).rearrange("p (g k u) -> p g u k", g=GROUPS, u=2)
+            nc.vector.tensor_copy(out=short_words[i][:, 0:2], in_=words[:, 0:2])
+            nc.scalar.copy(out=short_words[i][:, 2:4], in_=words[:, 2:4])
+
+        def short_transpose(i):
+            for two in range(GROUPS // 2):
+                bank = psum.tile([P, 2, 2, P], F32, name="bank")
+                words = short_wide[i][:].bitcast(F32)
+                for q in range(2):
+                    for u in range(2):
+                        g = 2 * two + q
+                        if i in ORDERED_TILES:
+                            piece = short_words[i][:, g, u, :]
+                        else:
+                            piece = words[:, 256 * g + u : 256 * (g + 1) : 2]
+                        nc.tensor.transpose(bank[:, q, u, :], piece, ident[:])
+                short_bank[(i, two)] = bank
+
+        def short_copy(i):
+            short_grouped[i] = work.tile([P, GROUPS, P, PACK], BF16, name="short_grouped", align_bytes=64)
+            for two in range(GROUPS // 2):
+                copy_words_out(short_grouped[i][:, 2 * two : 2 * two + 2], short_bank[(i, two)][:])
+
+        def short_quantise(i):
+            codes = work.tile([P, GROUPS, P], U32, name="short_codes", align_bytes=64, bufs=3)
+            scales = work.tile([P, GROUPS, P], U8, name="short_scales", align_bytes=64, bufs=3)
+            nc.vector.quantize_mx(
+                out=codes[:].rearrange("p g m -> p (g m)").bitcast(FP8X4),
+                scales=scales[:].rearrange("p g m -> p (g m)"),
+                in_=short_grouped[i][:].rearrange("p g m j -> p (g m j)"),
+            )
+            short_operand[i] = (codes, scales)
+
+        loss_bank = {}
+        loss_rows = {}
+
+        def loss_product(i, h, g0, g1):
+            codes, scales = short_operand[i]
+            if g0 == 0:
+                loss_bank[(i, h)] = psum.tile([P, HALF], F32, name="bank")
+            for g in range(g0, g1):
+                nc.tensor.matmul_mx(
+                    out=loss_bank[(i, h)][:],
+                    lhsT=codes[:, g, :].bitcast(FP8X4),
+                    lhsT_scale=scales[:, g, :],
+                    rhs=v_codes[g][:, half_cols(h)].bitcast(FP8X4),
+                    rhs_scale=v_scales[g][:, half_cols(h)],
+                    start=(g == 0),
+                    stop=(g == GROUPS - 1),
+                )
+
+        def loss_copy(i, h):
+            if h == 0:
+                loss_rows[i] = work.tile([P, S], F32, name="loss_rows", bufs=3)
+            if (i, h) == (BOOK_TILES - 1, 1):
+                nc.vector.tensor_copy(out=loss_rows[i][:, half_cols(h)], in_=loss_bank[(i, h)][:])
+            else:
+                nc.scalar.copy(out=loss_rows[i][:, half_cols(h)], in_=loss_bank[(i, h)][:])
+
+        def loss_store(i, cols):
+            nc.sync.dma_start(out=out[i * P : (i + 1) * P, cols], in_=loss_rows[i][:, cols])
+
+        calls = {}
+
+        def at(step, fn, *args):
+            calls.setdefault(step, []).append((fn, args))
+
+        def y_step(g, t, h):
+            return 8 * g + (2 * t + h if g in WIDE_GROUPS else 4 * h + t)
+
+        def sens_step(g, pair):
+            if g == 0:
+                return 4 * pair - 8
+            return 3 + 7 * (2 * (g - 1) + pair) // 2
+
+        def v_step(g, h):
+            if g in WIDE_GROUPS:
+                return y_step(g, PACK - 1, 1) + 6 + 4 * h
+            return y_step(g, PACK - 1, h) + 4
+
+        pairs = [(g, pair) for g in range(GROUPS) for pair in range(2)]
+        halves = [(g, h) for g in range(GROUPS) for h in range(2)]
+        banks = [(g, t, h) for g in range(GROUPS) for t in range(PACK) for h in range(2)]
+
+        at(-9, row_constants)
+        for g in range(F_PASSES):
+            at(2 * g - 8, shocks_interleave, g, 0)
+            at(-1, shocks_interleave, g, 1)
+        for g, t, h in banks:
+            at(y_step(g, t, h), y_product, g, t, h)
+        for g, pair in pairs:
+            for t in (2 * pair, 2 * pair + 1):
+                at(sens_step(g, pair), sens_transpose, g, t)
+        for i, step in enumerate((29, 32, 33)):
+            at(step, short_transpose, i)
+        for g, t, h in banks:
+            at(y_step(g, t, h), y_square, g, t, h)
+        for g, pair in pairs:
+            for t in (2 * pair, 2 * pair + 1):
+                at(sens_step(g, pair) + (1 if g == 0 else 0), sens_copy, g, t)
+        for i, step in enumerate((31, 34, 38)):
+            at(step, short_copy, i)
+        for g, t, h in banks:
+            if g not in WIDE_GROUPS:
+                at(y_step(g, t, h) + 2, v_clip, g, t, half_cols(h))
+            elif h == 1:
+                at(y_step(g, t, h) + 4, v_clip, g, t, slice(0, S))
+        for g in range(F_PASSES):
+            at(2 * g - 7, shocks_quantise, g, 0)
+            at(1, shocks_quantise, g, 1)
+        for g, pair in pairs:
+            at(sens_step(g, pair) + 2, sens_quantise, g, pair)
+        for i, step in enumerate((33, 36)):
+            at(step, short_quantise, i)
+        for g, h in halves:
+            at(v_step(g, h) + 4, v_quantise, g, h)
+        for g, h in halves:
+            at(v_step(g, h), v_interleave, g, h)
+        for i in range(3):
+            at(11 + 7 * i, short_widen, i)
+
+        for step in sorted(calls):
+            for fn, args in calls[step]:
+                fn(*args)
+
+        for i, h, g0, g1 in (
+            (0, 0, 0, 2), (0, 1, 0, 2), (0, 0, 2, 4), (1, 0, 0, 4), (1, 1, 0, 2), (0, 1, 2, 4), (1, 1, 2, 4)
+        ):
+            loss_product(i, h, g0, g1)
+        for i in range(BOOK_TILES + 1):
+            if i + 2 in ORDERED_TILES:
+                short_order(i + 2)
+            if 2 <= i < BOOK_TILES:
+                loss_product(i, 0, 0, GROUPS)
+                loss_product(i, 1, 0, GROUPS)
+            if i + 3 < BOOK_TILES:
+                short_widen(i + 3)
+            if 1 <= i < BOOK_TILES - 2:
+                short_transpose(i + 2)
+            if 1 <= i < BOOK_TILES:
+                loss_copy(i - 1, 0)
+                loss_copy(i - 1, 1)
+                loss_store(i - 1, slice(0, S))
+            if i == BOOK_TILES:
+                for h in range(2):
+                    loss_copy(i - 1, h)
+                    loss_store(i - 1, half_cols(h))
+            if 1 <= i < BOOK_TILES - 2:
+                short_copy(i + 2)
+            if i + 2 < BOOK_TILES:
+                short_quantise(i + 2)

@@ -23,12 +23,15 @@ GROUPS = N // K_PASS
 HALF = S // 2
 BOOK_TILES = B // P
 
-SHOCKS_SHARE = 384
-V_SHARE = {(1, 1): 0, (2, 0): 384, (2, 1): 384, (3, 0): 384, (3, 1): 0}
-
-WIDE_GROUPS = (1, 2)
-
-ORDERED_TILES = (5, 6, 7)
+GROUPED_BUFS = 3
+TURNED_BUFS = 3
+SQUARES_BUFS = 6
+V_ROWS_BUFS = 5
+WIDE_BUFS = 4
+SHORT_BUFS = 8
+LOSS_BUFS = 4
+HEAD_SHARE = 384
+LATE_SHARE = 128
 
 
 def tile_scenario_delta_gamma_losses_s7_kernel(
@@ -38,36 +41,21 @@ def tile_scenario_delta_gamma_losses_s7_kernel(
     with ExitStack() as ctx:
         keep = ctx.enter_context(tc.tile_pool(name="keep", bufs=1))
         work = ctx.enter_context(tc.tile_pool(name="work", bufs=2))
-        psum = ctx.enter_context(tc.psum_pool(name="psum", bufs=8))
-
-        warm = keep.tile([P, 1], F32, name="warm")
-        nc.vector.memset(warm[:], 0.0)
-        nc.scalar.activation(out=warm[:], in_=warm[:], func=ACT.Square)
-        ident = keep.tile([P, P], F32, name="ident")
-        make_identity(nc, ident[:])
-
-        tilt_raw = keep.tile([P, GROUPS, 16], BF16, name="tilt_raw")
-        cap_raw = keep.tile([P, GROUPS, 16], BF16, name="cap_raw")
-        nc.scalar.dma_start(out=tilt_raw[:, :, 0:PACK], in_=tilt.rearrange("(g m t) -> m g t", m=P, t=PACK))
-        nc.scalar.dma_start(out=cap_raw[:, :, 0:PACK], in_=cap.rearrange("(g m t) -> m g t", m=P, t=PACK))
-        half_tilt = keep.tile([P, GROUPS, PACK], F32, name="half_tilt")
-        half_tilt_sq = keep.tile([P, GROUPS, PACK], F32, name="half_tilt_sq")
-        cap_f32 = keep.tile([P, GROUPS, PACK], F32, name="cap_f32")
-
-        def row_constants():
-            nc.vector.tensor_scalar(
-                out=half_tilt[:], in0=tilt_raw[:, :, 0:PACK], scalar1=0.5, scalar2=None, op0=ALU.mult
-            )
-            nc.vector.tensor_copy(out=cap_f32[:], in_=cap_raw[:, :, 0:PACK])
-            nc.vector.tensor_tensor(out=half_tilt_sq[:], in0=half_tilt[:], in1=half_tilt[:], op=ALU.mult)
+        psum = ctx.enter_context(tc.psum_pool(name="psum", bufs=1))
+        ctx.enter_context(tc.manual_schedule())
 
         sens_view = sens.rearrange("(g m t) k -> g m t k", m=P, t=PACK)
         shocks_view = shocks.rearrange("(g p t) s -> g p t s", p=P, t=PACK)
         bytes_view = short_bytes.rearrange("(i p) k -> p i k", p=P)
         sens_rows = {}
         shocks_raw = {}
-        bytes_sb = keep.tile([P, BOOK_TILES, N], U8, name="bytes_sb")
-        scale_sb = keep.tile([P, N], F32, name="scale_sb")
+        bytes_rows = {}
+        scale_sb = keep.tile([P, GROUPS, 8], F32, name="scale_sb")
+        tilt_raw = keep.tile([P, GROUPS, 16], BF16, name="tilt_raw")
+        cap_raw = keep.tile([P, GROUPS, 16], BF16, name="cap_raw")
+
+        def half_cols(h):
+            return slice(h * HALF, (h + 1) * HALF)
 
         def load_sens(g, t0, n):
             rows = keep.tile([P, n, F], BF16, name="sens_rows_%d_%d" % (g, t0))
@@ -75,58 +63,60 @@ def tile_scenario_delta_gamma_losses_s7_kernel(
             for t in range(n):
                 sens_rows[(g, t0 + t)] = rows[:, t, :]
 
-        def load_shocks(g, h):
-            raw = keep.tile([P, PACK, HALF], BF16, name="shocks_raw_%d_%d" % (g, h))
-            nc.sync.dma_start(out=raw[:], in_=shocks_view[g][:, :, h * HALF : (h + 1) * HALF])
-            shocks_raw[(g, h)] = raw
+        def load_shocks(q, h):
+            raw = keep.tile([P, PACK, HALF], BF16, name="shocks_raw_%d_%d" % (q, h))
+            nc.sync.dma_start(out=raw[:], in_=shocks_view[q][:, :, half_cols(h)])
+            shocks_raw[(q, h)] = raw
 
-        def load_bytes(i0, i1):
-            nc.sync.dma_start(out=bytes_sb[:, i0:i1, :], in_=bytes_view[:, i0:i1, :])
+        def load_bytes(i0, n):
+            rows = keep.tile([P, n, N], U8, name="bytes_rows_%d" % i0)
+            nc.sync.dma_start(out=rows[:], in_=bytes_view[:, i0 : i0 + n, :])
+            for i in range(n):
+                bytes_rows[i0 + i] = rows[:, i, :]
 
-        load_shocks(0, 0)
-        load_sens(0, 0, 2)
-        load_shocks(1, 0)
-        load_sens(0, 2, 2)
-        load_shocks(0, 1)
-        load_shocks(1, 1)
-        load_sens(1, 0, 4)
-        load_sens(2, 0, 4)
-        nc.sync.dma_start(out=scale_sb[:], in_=short_scale.rearrange("o k -> (o k)").partition_broadcast(P))
-        load_bytes(0, 2)
-        load_sens(3, 0, 4)
-        load_bytes(2, 5)
-        load_bytes(5, 8)
+        def load_scale():
+            nc.scalar.dma_start(
+                out=scale_sb[:, :, 0:PACK], in_=short_scale.rearrange("o (g p t) -> p (o g) t", p=P, t=PACK)
+            )
 
-        ctx.enter_context(tc.manual_schedule())
+        def load_row_constants():
+            nc.scalar.dma_start(out=tilt_raw[:, :, 0:PACK], in_=tilt.rearrange("(g m t) -> m g t", m=P, t=PACK))
+            nc.scalar.dma_start(out=cap_raw[:, :, 0:PACK], in_=cap.rearrange("(g m t) -> m g t", m=P, t=PACK))
+
+        half_tilt = keep.tile([P, GROUPS, PACK], F32, name="half_tilt")
+        half_tilt_sq = keep.tile([P, GROUPS, PACK], F32, name="half_tilt_sq")
+        cap_f32 = keep.tile([P, GROUPS, PACK], F32, name="cap_f32")
+
+        def row_constants():
+            nc.scalar.activation(out=half_tilt[:], in_=tilt_raw[:, :, 0:PACK], func=ACT.Copy, scale=0.5)
+            nc.scalar.activation(out=half_tilt_sq[:], in_=tilt_raw[:, :, 0:PACK], func=ACT.Square, scale=0.5)
+            nc.scalar.copy(out=cap_f32[:], in_=cap_raw[:, :, 0:PACK])
 
         shocks_codes = keep.tile([P, F_PASSES, S], U32, name="shocks_codes", align_bytes=64)
         shocks_scales = keep.tile([P, F_PASSES, S], U8, name="shocks_scales", align_bytes=64)
         v_codes = [keep.tile([P, S], U32, name="v_codes_%d" % g, align_bytes=64) for g in range(GROUPS)]
         v_scales = [keep.tile([P, S], U8, name="v_scales_%d" % g, align_bytes=64) for g in range(GROUPS)]
 
-        def half_cols(h):
-            return slice(h * HALF, (h + 1) * HALF)
-
-        def interleave(dst, src, vector_cols):
-            d = dst.rearrange("p (b c) t -> p b t c", c=4)
-            s = src.rearrange("p t (b c) -> p b t c", c=4)
-            cut = vector_cols // 4
-            if cut > 0:
-                nc.vector.tensor_copy(out=d[:, 0:cut], in_=s[:, 0:cut])
-            if cut < HALF // 4:
-                nc.scalar.copy(out=d[:, cut:], in_=s[:, cut:])
+        def interleave(engine, dst, src, c0, c1):
+            d = dst.rearrange("p (b c) t -> p b t c", c=4)[:, c0 // 4 : c1 // 4]
+            s = src.rearrange("p t (b c) -> p b t c", c=4)[:, c0 // 4 : c1 // 4]
+            if engine == "vector":
+                nc.vector.tensor_copy(out=d, in_=s)
+            else:
+                nc.scalar.copy(out=d, in_=s)
 
         shocks_grouped = {}
 
-        def shocks_interleave(g, h):
-            shocks_grouped[(g, h)] = work.tile([P, HALF, PACK], BF16, name="shocks_grouped", align_bytes=64)
-            interleave(shocks_grouped[(g, h)][:], shocks_raw[(g, h)][:], SHOCKS_SHARE)
+        def shocks_interleave(q, h, engine, c0=0, c1=HALF):
+            if (q, h) not in shocks_grouped:
+                shocks_grouped[(q, h)] = work.tile([P, HALF, PACK], BF16, name="grouped", align_bytes=64, bufs=GROUPED_BUFS)
+            interleave(engine, shocks_grouped[(q, h)][:], shocks_raw[(q, h)][:], c0, c1)
 
-        def shocks_quantise(g, h):
+        def shocks_quantise(q, h):
             nc.vector.quantize_mx(
-                out=shocks_codes[:, g, half_cols(h)].bitcast(FP8X4),
-                scales=shocks_scales[:, g, half_cols(h)],
-                in_=shocks_grouped[(g, h)][:].rearrange("p n t -> p (n t)"),
+                out=shocks_codes[:, q, half_cols(h)].bitcast(FP8X4),
+                scales=shocks_scales[:, q, half_cols(h)],
+                in_=shocks_grouped[(q, h)][:].rearrange("p n t -> p (n t)"),
             )
 
         def copy_words_out(dst, bank):
@@ -140,8 +130,8 @@ def tile_scenario_delta_gamma_losses_s7_kernel(
         sens_grouped = {}
         sens_operand = {}
 
-        def sens_transpose(g, t):
-            sens_bank[(g, t)] = psum.tile([P, F_PASSES, 2, P], F32, name="bank")
+        def sens_transpose(g, t, bank):
+            sens_bank[(g, t)] = psum.tile([P, F_PASSES, 2, P], F32, name="bank_%d" % bank)
             words = sens_rows[(g, t)].bitcast(F32)
             for q in range(F_PASSES):
                 for u in range(2):
@@ -152,13 +142,13 @@ def tile_scenario_delta_gamma_losses_s7_kernel(
         def sens_copy(g, t):
             if t % 2 == 0:
                 sens_grouped[(g, t // 2)] = work.tile(
-                    [P, 2, F_PASSES, P, PACK], BF16, name="sens_grouped", align_bytes=64
+                    [P, 2, F_PASSES, P, PACK], BF16, name="turned", align_bytes=64, bufs=TURNED_BUFS
                 )
             copy_words_out(sens_grouped[(g, t // 2)][:, t % 2], sens_bank[(g, t)][:])
 
         def sens_quantise(g, pair):
-            codes = work.tile([P, 2, F_PASSES, P], U32, name="sens_codes", align_bytes=64, bufs=5)
-            scales = work.tile([P, 2, F_PASSES, P], U8, name="sens_scales", align_bytes=64, bufs=5)
+            codes = keep.tile([P, 2, F_PASSES, P], U32, name="sens_codes_%d_%d" % (g, pair), align_bytes=64)
+            scales = keep.tile([P, 2, F_PASSES, P], U8, name="sens_scales_%d_%d" % (g, pair), align_bytes=64)
             nc.vector.quantize_mx(
                 out=codes[:].rearrange("p a q m -> p (a q m)").bitcast(FP8X4),
                 scales=scales[:].rearrange("p a q m -> p (a q m)"),
@@ -171,9 +161,9 @@ def tile_scenario_delta_gamma_losses_s7_kernel(
         v_rows = {}
         v_grouped = {}
 
-        def y_product(g, t, h):
+        def y_product(g, t, h, bank):
             codes, scales = sens_operand[(g, t // 2)]
-            y_bank[(g, t, h)] = psum.tile([P, HALF], F32, name="bank")
+            y_bank[(g, t, h)] = psum.tile([P, HALF], F32, name="bank_%d" % bank)
             for q in range(F_PASSES):
                 nc.tensor.matmul_mx(
                     out=y_bank[(g, t, h)][:],
@@ -186,30 +176,30 @@ def tile_scenario_delta_gamma_losses_s7_kernel(
                 )
 
         def y_square(g, t, h):
-            if (g, t) not in squares:
-                squares[(g, t)] = work.tile([P, S], F32, name="squares", bufs=5)
+            squares[(g, t, h)] = work.tile([P, HALF], F32, name="squares", bufs=SQUARES_BUFS)
             nc.scalar.activation(
-                out=squares[(g, t)][:, half_cols(h)],
+                out=squares[(g, t, h)][:],
                 in_=y_bank[(g, t, h)][:],
                 func=ACT.Square,
                 bias=half_tilt[:, g, t : t + 1],
             )
 
-        def v_clip(g, t, cols):
-            if g not in v_rows:
-                v_rows[g] = work.tile([P, PACK, S], BF16, name="v_rows")
+        def v_clip(g, t, h):
+            if (g, h) not in v_rows:
+                v_rows[(g, h)] = work.tile([P, PACK, HALF], BF16, name="v_rows", bufs=V_ROWS_BUFS)
             nc.vector.tensor_scalar(
-                out=v_rows[g][:, t, cols],
-                in0=squares[(g, t)][:, cols],
+                out=v_rows[(g, h)][:, t, :],
+                in0=squares[(g, t, h)][:],
                 scalar1=half_tilt_sq[:, g, t : t + 1],
                 scalar2=cap_f32[:, g, t : t + 1],
                 op0=ALU.subtract,
                 op1=ALU.min,
             )
 
-        def v_interleave(g, h):
-            v_grouped[(g, h)] = work.tile([P, HALF, PACK], BF16, name="v_grouped", align_bytes=64, bufs=3)
-            interleave(v_grouped[(g, h)][:], v_rows[g][:, :, half_cols(h)], V_SHARE.get((g, h), HALF))
+        def v_interleave(g, h, engine, c0=0, c1=HALF):
+            if (g, h) not in v_grouped:
+                v_grouped[(g, h)] = work.tile([P, HALF, PACK], BF16, name="grouped", align_bytes=64, bufs=GROUPED_BUFS)
+            interleave(engine, v_grouped[(g, h)][:], v_rows[(g, h)][:], c0, c1)
 
         def v_quantise(g, h):
             nc.vector.quantize_mx(
@@ -219,59 +209,74 @@ def tile_scenario_delta_gamma_losses_s7_kernel(
             )
 
         short_wide = {}
-        short_words = {}
+        short_ordered = set()
         short_bank = {}
         short_grouped = {}
         short_operand = {}
 
-        def short_widen(i):
-            short_wide[i] = work.tile([P, N], BF16, name="short_wide", bufs=3)
+        def short_cast(i, engine, two0=0, two1=2):
+            if i not in short_wide:
+                short_wide[i] = work.tile([P, 2, 2 * K_PASS], BF16, name="short_wide", bufs=WIDE_BUFS)
+            codes = bytes_rows[i].bitcast(FP8)
+            if engine == "vector":
+                for two in range(two0, two1):
+                    nc.vector.tensor_scalar(
+                        out=short_wide[i][:, two, :].rearrange("p (u m e) -> p m u e", u=2, e=2),
+                        in0=codes[:, 2 * two * K_PASS : 2 * (two + 1) * K_PASS].rearrange("p (m u e) -> p m u e", u=2, e=2),
+                        scalar1=one[:],
+                        scalar2=None,
+                        op0=ALU.mult,
+                    )
+                    short_ordered.add((i, two))
+            else:
+                nc.scalar.copy(
+                    out=short_wide[i][:, two0:two1, :].rearrange("p a k -> p (a k)"),
+                    in_=codes[:, 2 * two0 * K_PASS : 2 * two1 * K_PASS],
+                )
+
+        def short_transpose(i, two, bank):
+            short_bank[(i, two)] = psum.tile([P, 2, 2, P], F32, name="bank_%d" % bank)
+            words = short_wide[i][:, two, :].bitcast(F32)
+            for q in range(2):
+                for u in range(2):
+                    if (i, two) in short_ordered:
+                        piece = words[:, 256 * u + P * q : 256 * u + P * (q + 1)]
+                    else:
+                        piece = words[:, 256 * q + u : 256 * (q + 1) : 2]
+                    nc.tensor.transpose(short_bank[(i, two)][:, u, q, :], piece, ident[:])
+
+        def short_scale_out(i, two):
+            if two == 0:
+                short_grouped[i] = work.tile([P, GROUPS, P, PACK], BF16, name="short_grouped", align_bytes=64)
+            passes = slice(2 * two, 2 * two + 2)
+            values = short_bank[(i, two)][:].rearrange("p u q m -> p (u q m)").bitcast(BF16)
+            factors = scale_sb[:, passes, 0:PACK].rearrange("p q (u e) -> p q u e", u=2)
             nc.vector.tensor_tensor(
-                out=short_wide[i][:], in0=bytes_sb[:, i, :].bitcast(FP8), in1=scale_sb[:], op=ALU.mult
+                out=short_grouped[i][:, passes].rearrange("p q m (u e) -> p q m u e", u=2),
+                in0=values.rearrange("p (u q m e) -> p q m u e", u=2, q=2, e=2),
+                in1=factors.unsqueeze(2).to_broadcast([P, 2, P, 2, 2]),
+                op=ALU.mult,
             )
 
-        def short_order(i):
-            short_words[i] = work.tile([P, GROUPS, 2, P], F32, name="short_words")
-            words = short_wide[i][:].bitcast(F32).rearrange("p (g k u) -> p g u k", g=GROUPS, u=2)
-            nc.vector.tensor_copy(out=short_words[i][:, 0:2], in_=words[:, 0:2])
-            nc.scalar.copy(out=short_words[i][:, 2:4], in_=words[:, 2:4])
-
-        def short_transpose(i):
-            for two in range(GROUPS // 2):
-                bank = psum.tile([P, 2, 2, P], F32, name="bank")
-                words = short_wide[i][:].bitcast(F32)
-                for q in range(2):
-                    for u in range(2):
-                        g = 2 * two + q
-                        if i in ORDERED_TILES:
-                            piece = short_words[i][:, g, u, :]
-                        else:
-                            piece = words[:, 256 * g + u : 256 * (g + 1) : 2]
-                        nc.tensor.transpose(bank[:, q, u, :], piece, ident[:])
-                short_bank[(i, two)] = bank
-
-        def short_copy(i):
-            short_grouped[i] = work.tile([P, GROUPS, P, PACK], BF16, name="short_grouped", align_bytes=64)
-            for two in range(GROUPS // 2):
-                copy_words_out(short_grouped[i][:, 2 * two : 2 * two + 2], short_bank[(i, two)][:])
-
-        def short_quantise(i):
-            codes = work.tile([P, GROUPS, P], U32, name="short_codes", align_bytes=64, bufs=3)
-            scales = work.tile([P, GROUPS, P], U8, name="short_scales", align_bytes=64, bufs=3)
+        def short_quantise(i, g0=0, g1=GROUPS):
+            if i not in short_operand:
+                codes = work.tile([P, GROUPS, P], U32, name="short_codes", align_bytes=64, bufs=SHORT_BUFS)
+                scales = work.tile([P, GROUPS, P], U8, name="short_scales", align_bytes=64, bufs=SHORT_BUFS)
+                short_operand[i] = (codes, scales)
+            codes, scales = short_operand[i]
             nc.vector.quantize_mx(
-                out=codes[:].rearrange("p g m -> p (g m)").bitcast(FP8X4),
-                scales=scales[:].rearrange("p g m -> p (g m)"),
-                in_=short_grouped[i][:].rearrange("p g m j -> p (g m j)"),
+                out=codes[:, g0:g1].rearrange("p g m -> p (g m)").bitcast(FP8X4),
+                scales=scales[:, g0:g1].rearrange("p g m -> p (g m)"),
+                in_=short_grouped[i][:, g0:g1].rearrange("p g m j -> p (g m j)"),
             )
-            short_operand[i] = (codes, scales)
 
         loss_bank = {}
         loss_rows = {}
 
-        def loss_product(i, h, g0, g1):
+        def loss_product(i, h, bank, g0=0, g1=GROUPS):
             codes, scales = short_operand[i]
             if g0 == 0:
-                loss_bank[(i, h)] = psum.tile([P, HALF], F32, name="bank")
+                loss_bank[(i, h)] = psum.tile([P, HALF], F32, name="bank_%d" % bank)
             for g in range(g0, g1):
                 nc.tensor.matmul_mx(
                     out=loss_bank[(i, h)][:],
@@ -283,103 +288,164 @@ def tile_scenario_delta_gamma_losses_s7_kernel(
                     stop=(g == GROUPS - 1),
                 )
 
-        def loss_copy(i, h):
-            if h == 0:
-                loss_rows[i] = work.tile([P, S], F32, name="loss_rows", bufs=3)
-            if (i, h) == (BOOK_TILES - 1, 1):
-                nc.vector.tensor_copy(out=loss_rows[i][:, half_cols(h)], in_=loss_bank[(i, h)][:])
+        def loss_out(i, h, engine="scalar"):
+            rows = work.tile([P, HALF], F32, name="loss_rows", bufs=LOSS_BUFS)
+            if engine == "vector":
+                nc.vector.tensor_copy(out=rows[:], in_=loss_bank[(i, h)][:])
             else:
-                nc.scalar.copy(out=loss_rows[i][:, half_cols(h)], in_=loss_bank[(i, h)][:])
+                nc.scalar.copy(out=rows[:], in_=loss_bank[(i, h)][:])
+            nc.sync.dma_start(out=out[i * P : (i + 1) * P, half_cols(h)], in_=rows[:])
 
-        def loss_store(i, cols):
-            nc.sync.dma_start(out=out[i * P : (i + 1) * P, cols], in_=loss_rows[i][:, cols])
 
-        calls = {}
+        one = keep.tile([P, 1], F32, name="one")
+        nc.vector.memset(one[:], 1.0)
+        ident = keep.tile([P, P], F32, name="ident")
+        make_identity(nc, ident[:])
 
-        def at(step, fn, *args):
-            calls.setdefault(step, []).append((fn, args))
+        load_scale()
+        load_row_constants()
+        load_bytes(0, 1)
+        load_bytes(1, 1)
+        load_shocks(0, 0)
+        load_sens(0, 0, 2)
+        load_shocks(1, 0)
+        load_sens(0, 2, 2)
+        load_bytes(2, 1)
+        load_sens(1, 0, 2)
+        load_sens(1, 2, 2)
+        load_bytes(3, 1)
+        load_shocks(0, 1)
+        load_sens(2, 0, 2)
+        load_sens(2, 2, 2)
+        load_shocks(1, 1)
+        load_sens(3, 0, 4)
+        load_bytes(4, 4)
 
-        def y_step(g, t, h):
-            return 8 * g + (2 * t + h if g in WIDE_GROUPS else 4 * h + t)
+        def turn_sens(g, tiles, bank):
+            for n, t in enumerate(tiles):
+                sens_transpose(g, t, bank + n)
+                sens_copy(g, t)
 
-        def sens_step(g, pair):
+        def turn_short(i, bank):
+            for two in range(2):
+                short_transpose(i, two, bank + two)
+
+        def y_tiles(g, tiles, h, bank):
+            for n, t in enumerate(tiles):
+                y_product(g, t, h, bank + n)
+                y_square(g, t, h)
+
+        def clip_tiles(g, tiles, h):
+            for t in tiles:
+                v_clip(g, t, h)
+
+        for i in range(2):
+            short_cast(i, "vector", 0, 1)
+            short_cast(i, "scalar", 1, 2)
+        short_transpose(0, 0, 0)
+        short_transpose(1, 0, 1)
+        short_transpose(0, 1, 2)
+        short_transpose(1, 1, 3)
+        row_constants()
+        shocks_interleave(0, 0, "scalar")
+        short_scale_out(0, 0)
+        short_scale_out(1, 0)
+        turn_sens(0, (0, 1), 4)
+        short_scale_out(0, 1)
+        shocks_interleave(1, 0, "vector", 0, HEAD_SHARE)
+        shocks_interleave(1, 0, "scalar", HEAD_SHARE, HALF)
+        shocks_quantise(0, 0)
+        sens_quantise(0, 0)
+        shocks_quantise(1, 0)
+        turn_sens(0, (2, 3), 6)
+        short_cast(2, "scalar")
+        short_scale_out(1, 1)
+        sens_quantise(0, 1)
+        short_quantise(0)
+        for u in range(8):
+            g, pair = divmod(u, 2)
+            tiles = (2 * pair, 2 * pair + 1)
+            y_tiles(g, tiles, 0, 2 * (u % 2))
+            if u + 2 < 8:
+                turn_sens(g + 1, tiles, 4 + 2 * pair)
+            else:
+                turn_short(u - 4, 4 + 2 * pair)
+            if u == 0:
+                short_quantise(1)
+            if u in (0, 2):
+                shocks_interleave(u // 2, 1, "vector")
+            if u in (1, 3):
+                shocks_quantise(u // 2, 1)
+            if u == 4:
+                short_cast(3, "vector")
+            if u == 5:
+                v_interleave(0, 0, "vector")
+            clip_tiles(g, tiles, 0)
+            if u + 2 < 8:
+                sens_quantise(g + 1, pair)
+            else:
+                if u == 6:
+                    v_quantise(0, 0)
+                    v_interleave(1, 0, "scalar")
+                short_scale_out(u - 4, 0)
+                short_scale_out(u - 4, 1)
+        short_quantise(2)
+        v_quantise(1, 0)
+        short_quantise(3)
+        for g in range(GROUPS):
+            y_tiles(g, range(4), 1, 0)
+            late = (g + 2, 0) if g + 2 < GROUPS else (g - 2, 1)
+            v_interleave(*late, "scalar" if g == 0 else "vector")
+            clip_tiles(g, (0, 1), 1)
+            if g > 0:
+                v_quantise(*late)
+            if g < 3:
+                clip_tiles(g, (2, 3), 1)
             if g == 0:
-                return 4 * pair - 8
-            return 3 + 7 * (2 * (g - 1) + pair) // 2
-
-        def v_step(g, h):
-            if g in WIDE_GROUPS:
-                return y_step(g, PACK - 1, 1) + 6 + 4 * h
-            return y_step(g, PACK - 1, h) + 4
-
-        pairs = [(g, pair) for g in range(GROUPS) for pair in range(2)]
-        halves = [(g, h) for g in range(GROUPS) for h in range(2)]
-        banks = [(g, t, h) for g in range(GROUPS) for t in range(PACK) for h in range(2)]
-
-        at(-9, row_constants)
-        for g in range(F_PASSES):
-            at(2 * g - 8, shocks_interleave, g, 0)
-            at(-1, shocks_interleave, g, 1)
-        for g, t, h in banks:
-            at(y_step(g, t, h), y_product, g, t, h)
-        for g, pair in pairs:
-            for t in (2 * pair, 2 * pair + 1):
-                at(sens_step(g, pair), sens_transpose, g, t)
-        for i, step in enumerate((29, 32, 33)):
-            at(step, short_transpose, i)
-        for g, t, h in banks:
-            at(y_step(g, t, h), y_square, g, t, h)
-        for g, pair in pairs:
-            for t in (2 * pair, 2 * pair + 1):
-                at(sens_step(g, pair) + (1 if g == 0 else 0), sens_copy, g, t)
-        for i, step in enumerate((31, 34, 38)):
-            at(step, short_copy, i)
-        for g, t, h in banks:
-            if g not in WIDE_GROUPS:
-                at(y_step(g, t, h) + 2, v_clip, g, t, half_cols(h))
-            elif h == 1:
-                at(y_step(g, t, h) + 4, v_clip, g, t, slice(0, S))
-        for g in range(F_PASSES):
-            at(2 * g - 7, shocks_quantise, g, 0)
-            at(1, shocks_quantise, g, 1)
-        for g, pair in pairs:
-            at(sens_step(g, pair) + 2, sens_quantise, g, pair)
-        for i, step in enumerate((33, 36)):
-            at(step, short_quantise, i)
-        for g, h in halves:
-            at(v_step(g, h) + 4, v_quantise, g, h)
-        for g, h in halves:
-            at(v_step(g, h), v_interleave, g, h)
-        for i in range(3):
-            at(11 + 7 * i, short_widen, i)
-
-        for step in sorted(calls):
-            for fn, args in calls[step]:
-                fn(*args)
-
-        for i, h, g0, g1 in (
-            (0, 0, 0, 2), (0, 1, 0, 2), (0, 0, 2, 4), (1, 0, 0, 4), (1, 1, 0, 2), (0, 1, 2, 4), (1, 1, 2, 4)
-        ):
-            loss_product(i, h, g0, g1)
-        for i in range(BOOK_TILES + 1):
-            if i + 2 in ORDERED_TILES:
-                short_order(i + 2)
-            if 2 <= i < BOOK_TILES:
-                loss_product(i, 0, 0, GROUPS)
-                loss_product(i, 1, 0, GROUPS)
-            if i + 3 < BOOK_TILES:
-                short_widen(i + 3)
-            if 1 <= i < BOOK_TILES - 2:
-                short_transpose(i + 2)
-            if 1 <= i < BOOK_TILES:
-                loss_copy(i - 1, 0)
-                loss_copy(i - 1, 1)
-                loss_store(i - 1, slice(0, S))
-            if i == BOOK_TILES:
-                for h in range(2):
-                    loss_copy(i - 1, h)
-                    loss_store(i - 1, half_cols(h))
-            if 1 <= i < BOOK_TILES - 2:
-                short_copy(i + 2)
-            if i + 2 < BOOK_TILES:
-                short_quantise(i + 2)
+                v_quantise(*late)
+            if g in (1, 2):
+                short_cast(3 + g, "scalar")
+            for gg in ((), (0, 1), (2,), (3,))[g]:
+                for i in range(4):
+                    loss_product(i, 0, 4 + i, gg, gg + 1)
+        turn_short(4, 0)
+        turn_short(5, 2)
+        for i in range(4):
+            loss_out(i, 0)
+        v_interleave(2, 1, "scalar")
+        short_scale_out(4, 0)
+        short_scale_out(4, 1)
+        clip_tiles(3, (2, 3), 1)
+        short_quantise(4)
+        short_cast(6, "scalar")
+        v_interleave(3, 1, "scalar", LATE_SHARE, HALF)
+        for i in range(4):
+            loss_product(i, 1, 4 + i, 0, 2)
+        short_scale_out(5, 0)
+        v_quantise(2, 1)
+        short_scale_out(5, 1)
+        v_interleave(3, 1, "vector", 0, LATE_SHARE)
+        loss_product(4, 0, 0)
+        loss_out(4, 0)
+        for i in range(4):
+            loss_product(i, 1, 4 + i, 2, 3)
+        v_quantise(3, 1)
+        short_quantise(5)
+        short_cast(7, "vector")
+        turn_short(6, 1)
+        for i in range(4):
+            loss_product(i, 1, 4 + i, 3, 4)
+            loss_out(i, 1)
+        short_transpose(7, 0, 3)
+        short_transpose(7, 1, 0)
+        short_scale_out(6, 0)
+        short_scale_out(6, 1)
+        short_scale_out(7, 0)
+        short_quantise(6)
+        short_scale_out(7, 1)
+        short_quantise(7, 0, 2)
+        short_quantise(7, 2, 4)
+        rest = [(4, 1), (5, 0), (5, 1), (6, 0), (6, 1), (7, 0), (7, 1)]
+        for n, (i, h) in enumerate(rest):
+            loss_product(i, h, (4 + n) % 8)
+            loss_out(i, h, "vector" if (i, h) == (7, 1) else "scalar")

@@ -80,8 +80,8 @@ def tile_scenario_delta_gamma_losses_s7_kernel(
             )
 
         def load_row_constants():
-            nc.scalar.dma_start(out=tilt_raw[:, :, 0:PACK], in_=tilt.rearrange("(g m t) -> m g t", m=P, t=PACK))
-            nc.scalar.dma_start(out=cap_raw[:, :, 0:PACK], in_=cap.rearrange("(g m t) -> m g t", m=P, t=PACK))
+            nc.gpsimd.dma_start(out=tilt_raw[:, :, 0:PACK], in_=tilt.rearrange("(g m t) -> m g t", m=P, t=PACK))
+            nc.gpsimd.dma_start(out=cap_raw[:, :, 0:PACK], in_=cap.rearrange("(g m t) -> m g t", m=P, t=PACK))
 
         half_tilt = keep.tile([P, GROUPS, PACK], F32, name="half_tilt")
         half_tilt_sq = keep.tile([P, GROUPS, PACK], F32, name="half_tilt_sq")
@@ -271,30 +271,30 @@ def tile_scenario_delta_gamma_losses_s7_kernel(
             )
 
         loss_bank = {}
-        loss_rows = {}
 
-        def loss_product(i, h, bank, g0=0, g1=GROUPS):
+        def loss_product(i, c0, width, bank, g0=0, g1=GROUPS):
             codes, scales = short_operand[i]
+            cols = slice(c0, c0 + width)
             if g0 == 0:
-                loss_bank[(i, h)] = psum.tile([P, HALF], F32, name="bank_%d" % bank)
+                loss_bank[(i, c0)] = psum.tile([P, width], F32, name="bank_%d" % bank)
             for g in range(g0, g1):
                 nc.tensor.matmul_mx(
-                    out=loss_bank[(i, h)][:],
+                    out=loss_bank[(i, c0)][:],
                     lhsT=codes[:, g, :].bitcast(FP8X4),
                     lhsT_scale=scales[:, g, :],
-                    rhs=v_codes[g][:, half_cols(h)].bitcast(FP8X4),
-                    rhs_scale=v_scales[g][:, half_cols(h)],
+                    rhs=v_codes[g][:, cols].bitcast(FP8X4),
+                    rhs_scale=v_scales[g][:, cols],
                     start=(g == 0),
                     stop=(g == GROUPS - 1),
                 )
 
-        def loss_out(i, h, engine="scalar"):
-            rows = work.tile([P, HALF], F32, name="loss_rows", bufs=LOSS_BUFS)
+        def loss_out(i, c0, width, engine="scalar"):
+            rows = work.tile([P, width], F32, name="loss_rows", bufs=LOSS_BUFS)
             if engine == "vector":
-                nc.vector.tensor_copy(out=rows[:], in_=loss_bank[(i, h)][:])
+                nc.vector.tensor_copy(out=rows[:], in_=loss_bank[(i, c0)][:])
             else:
-                nc.scalar.copy(out=rows[:], in_=loss_bank[(i, h)][:])
-            nc.sync.dma_start(out=out[i * P : (i + 1) * P, half_cols(h)], in_=rows[:])
+                nc.scalar.copy(out=rows[:], in_=loss_bank[(i, c0)][:])
+            nc.sync.dma_start(out=out[i * P : (i + 1) * P, c0 : c0 + width], in_=rows[:])
 
 
         one = keep.tile([P, 1], F32, name="one")
@@ -407,11 +407,11 @@ def tile_scenario_delta_gamma_losses_s7_kernel(
                 short_cast(3 + g, "scalar")
             for gg in ((), (0, 1), (2,), (3,))[g]:
                 for i in range(4):
-                    loss_product(i, 0, 4 + i, gg, gg + 1)
+                    loss_product(i, 0, HALF, 4 + i, gg, gg + 1)
         turn_short(4, 0)
         turn_short(5, 2)
         for i in range(4):
-            loss_out(i, 0)
+            loss_out(i, 0, HALF)
         v_interleave(2, 1, "scalar")
         short_scale_out(4, 0)
         short_scale_out(4, 1)
@@ -420,32 +420,37 @@ def tile_scenario_delta_gamma_losses_s7_kernel(
         short_cast(6, "scalar")
         v_interleave(3, 1, "scalar", LATE_SHARE, HALF)
         for i in range(4):
-            loss_product(i, 1, 4 + i, 0, 2)
+            loss_product(i, HALF, HALF, 4 + i, 0, 2)
         short_scale_out(5, 0)
         v_quantise(2, 1)
         short_scale_out(5, 1)
         v_interleave(3, 1, "vector", 0, LATE_SHARE)
-        loss_product(4, 0, 0)
-        loss_out(4, 0)
+        loss_product(4, 0, HALF, 0)
+        loss_out(4, 0, HALF)
         for i in range(4):
-            loss_product(i, 1, 4 + i, 2, 3)
-        v_quantise(3, 1)
+            loss_product(i, HALF, HALF, 4 + i, 2, 3)
         short_quantise(5)
         short_cast(7, "vector")
         turn_short(6, 1)
+        v_quantise(3, 1)
+        loss_product(4, HALF, HALF, 3, 0, 3)
         for i in range(4):
-            loss_product(i, 1, 4 + i, 3, 4)
-            loss_out(i, 1)
-        short_transpose(7, 0, 3)
-        short_transpose(7, 1, 0)
+            loss_product(i, HALF, HALF, 4 + i, 3, 4)
+            loss_out(i, HALF, HALF)
+        loss_product(4, HALF, HALF, 3, 3, 4)
+        short_transpose(7, 0, 0)
+        short_transpose(7, 1, 4)
+        loss_out(4, HALF, HALF)
         short_scale_out(6, 0)
         short_scale_out(6, 1)
+        short_quantise(6, 0, 2)
+        short_quantise(6, 2, 4)
         short_scale_out(7, 0)
-        short_quantise(6)
         short_scale_out(7, 1)
         short_quantise(7, 0, 2)
         short_quantise(7, 2, 4)
-        rest = [(4, 1), (5, 0), (5, 1), (6, 0), (6, 1), (7, 0), (7, 1)]
-        for n, (i, h) in enumerate(rest):
-            loss_product(i, h, (4 + n) % 8)
-            loss_out(i, h, "vector" if (i, h) == (7, 1) else "scalar")
+        rest = [(5, 0, HALF), (5, HALF, HALF), (6, 0, HALF), (6, HALF, HALF), (7, 0, HALF)]
+        rest = rest + [(7, HALF, HALF // 2), (7, 3 * HALF // 2, HALF // 2)]
+        for n, (i, c0, width) in enumerate(rest):
+            loss_product(i, c0, width, (5 + n) % 8)
+            loss_out(i, c0, width, "vector" if n == 5 else "scalar")

@@ -80,8 +80,8 @@ def tile_scenario_delta_gamma_losses_s7_kernel(
             )
 
         def load_row_constants():
-            nc.gpsimd.dma_start(out=tilt_raw[:, :, 0:PACK], in_=tilt.rearrange("(g m t) -> m g t", m=P, t=PACK))
-            nc.gpsimd.dma_start(out=cap_raw[:, :, 0:PACK], in_=cap.rearrange("(g m t) -> m g t", m=P, t=PACK))
+            nc.scalar.dma_start(out=tilt_raw[:, :, 0:PACK], in_=tilt.rearrange("(g m t) -> m g t", m=P, t=PACK))
+            nc.scalar.dma_start(out=cap_raw[:, :, 0:PACK], in_=cap.rearrange("(g m t) -> m g t", m=P, t=PACK))
 
         half_tilt = keep.tile([P, GROUPS, PACK], F32, name="half_tilt")
         half_tilt_sq = keep.tile([P, GROUPS, PACK], F32, name="half_tilt_sq")
@@ -396,61 +396,73 @@ def tile_scenario_delta_gamma_losses_s7_kernel(
             y_tiles(g, range(4), 1, 0)
             late = (g + 2, 0) if g + 2 < GROUPS else (g - 2, 1)
             v_interleave(*late, "scalar" if g == 0 else "vector")
-            clip_tiles(g, (0, 1), 1)
+            if g < 3:
+                clip_tiles(g, (0, 1), 1)
             if g > 0:
                 v_quantise(*late)
             if g < 3:
                 clip_tiles(g, (2, 3), 1)
             if g == 0:
                 v_quantise(*late)
-            if g in (1, 2):
-                short_cast(3 + g, "scalar")
-            for gg in ((), (0, 1), (2,), (3,))[g]:
+            if g == 1:
+                short_cast(4, "scalar")
+            for gg in ((), (0, 1), (2, 3), ())[g]:
                 for i in range(4):
                     loss_product(i, 0, HALF, 4 + i, gg, gg + 1)
-        turn_short(4, 0)
-        turn_short(5, 2)
-        for i in range(4):
-            loss_out(i, 0, HALF)
-        v_interleave(2, 1, "scalar")
+            if g == 2:
+                loss_out(0, 0, HALF)
+                loss_out(1, 0, HALF)
+                short_cast(5, "scalar")
+                loss_out(2, 0, HALF)
+                loss_out(3, 0, HALF)
+        held = [6, 7, 2, 3, 5]
+        turn_short(4, 4)
         short_scale_out(4, 0)
         short_scale_out(4, 1)
-        clip_tiles(3, (2, 3), 1)
-        short_quantise(4)
+        v_interleave(2, 1, "scalar")
+        for i in range(2):
+            loss_product(i, HALF, HALF, held[i], 0, 2)
+        turn_short(5, 0)
+        short_quantise(4, 0, 2)
+        short_quantise(4, 2, 4)
+        clip_tiles(3, range(4), 1)
+        for i in range(2, 4):
+            loss_product(i, HALF, HALF, held[i], 0, 2)
+        loss_product(4, 0, HALF, 4)
+        loss_product(4, HALF, HALF, held[4], 0, 2)
         short_cast(6, "scalar")
+        loss_out(4, 0, HALF)
         v_interleave(3, 1, "scalar", LATE_SHARE, HALF)
-        for i in range(4):
-            loss_product(i, HALF, HALF, 4 + i, 0, 2)
         short_scale_out(5, 0)
         v_quantise(2, 1)
         short_scale_out(5, 1)
         v_interleave(3, 1, "vector", 0, LATE_SHARE)
-        loss_product(4, 0, HALF, 0)
-        loss_out(4, 0, HALF)
-        for i in range(4):
-            loss_product(i, HALF, HALF, 4 + i, 2, 3)
         short_quantise(5)
         short_cast(7, "vector")
-        turn_short(6, 1)
+        for i in range(5):
+            loss_product(i, HALF, HALF, held[i], 2, 3)
+        turn_short(6, 0)
+        loss_product(5, 0, HALF, 4)
+        loss_out(5, 0, HALF)
         v_quantise(3, 1)
-        loss_product(4, HALF, HALF, 3, 0, 3)
-        for i in range(4):
-            loss_product(i, HALF, HALF, 4 + i, 3, 4)
+        for i in range(5):
+            loss_product(i, HALF, HALF, held[i], 3, 4)
             loss_out(i, HALF, HALF)
-        loss_product(4, HALF, HALF, 3, 3, 4)
-        short_transpose(7, 0, 0)
-        short_transpose(7, 1, 4)
-        loss_out(4, HALF, HALF)
-        short_scale_out(6, 0)
-        short_scale_out(6, 1)
-        short_quantise(6, 0, 2)
-        short_quantise(6, 2, 4)
-        short_scale_out(7, 0)
-        short_scale_out(7, 1)
-        short_quantise(7, 0, 2)
-        short_quantise(7, 2, 4)
-        rest = [(5, 0, HALF), (5, HALF, HALF), (6, 0, HALF), (6, HALF, HALF), (7, 0, HALF)]
-        rest = rest + [(7, HALF, HALF // 2), (7, 3 * HALF // 2, HALF // 2)]
-        for n, (i, c0, width) in enumerate(rest):
-            loss_product(i, c0, width, (5 + n) % 8)
-            loss_out(i, c0, width, "vector" if n == 5 else "scalar")
+        short_transpose(7, 0, 4)
+        short_transpose(7, 1, 6)
+        for i in (6, 7):
+            short_scale_out(i, 0)
+            short_scale_out(i, 1)
+            short_quantise(i, 0, 2)
+            short_quantise(i, 2, 4)
+        loss_product(5, HALF, HALF, 7)
+        loss_out(5, HALF, HALF)
+        for h in range(2):
+            loss_product(6, h * HALF, HALF, 2 + h)
+            loss_out(6, h * HALF, HALF)
+        last = [(0, HALF), (HALF, HALF // 2), (3 * HALF // 2, HALF // 2)]
+        for n, (c0, width) in enumerate(last):
+            loss_product(7, c0, width, (5, 0, 1)[n], 0, 2)
+        for n, (c0, width) in enumerate(last):
+            loss_product(7, c0, width, (5, 0, 1)[n], 2, 4)
+            loss_out(7, c0, width, "vector" if n == 1 else "scalar")

@@ -30,8 +30,16 @@ V_ROWS_BUFS = 5
 WIDE_BUFS = 4
 SHORT_BUFS = 8
 LOSS_BUFS = 4
-HEAD_SHARE = 384
-LATE_SHARE = 128
+HEAD_SHARE = 320
+W3 = "scalar"
+W3_AT = 6
+I_AT = 3
+W7 = "scalar"
+S_TURNS = (0,)
+LATE_SHARE = 0
+PASSES = ((), (0, 1), (2, 3), ())
+VQ_AT = 4
+W6 = "scalar"
 
 
 def tile_scenario_delta_gamma_losses_s7_kernel(
@@ -376,43 +384,42 @@ def tile_scenario_delta_gamma_losses_s7_kernel(
                 shocks_interleave(u // 2, 1, "vector")
             if u in (1, 3):
                 shocks_quantise(u // 2, 1)
-            if u == 4:
-                short_cast(3, "vector")
-            if u == 5:
-                v_interleave(0, 0, "vector")
+            if u == W3_AT:
+                short_cast(3, W3)
+            if u in (I_AT, I_AT + 2):
+                v_interleave((u - I_AT) // 2, 0, "vector")
+            if u in (I_AT + 1, I_AT + 3):
+                v_quantise((u - I_AT) // 2, 0)
             clip_tiles(g, tiles, 0)
             if u + 2 < 8:
                 sens_quantise(g + 1, pair)
             else:
-                if u == 6:
-                    v_quantise(0, 0)
-                    v_interleave(1, 0, "scalar")
+                if u == 7:
+                    short_quantise(2)
                 short_scale_out(u - 4, 0)
                 short_scale_out(u - 4, 1)
-        short_quantise(2)
-        v_quantise(1, 0)
+        short_cast(4, "scalar")
         short_quantise(3)
         for g in range(GROUPS):
             y_tiles(g, range(4), 1, 0)
             late = (g + 2, 0) if g + 2 < GROUPS else (g - 2, 1)
-            v_interleave(*late, "scalar" if g == 0 else "vector")
+            v_interleave(*late, "scalar" if g in S_TURNS else "vector")
             if g < 3:
                 clip_tiles(g, (0, 1), 1)
-            if g > 0:
+            if g not in S_TURNS or g == 3:
                 v_quantise(*late)
             if g < 3:
                 clip_tiles(g, (2, 3), 1)
-            if g == 0:
+            if g in S_TURNS and g < 3:
                 v_quantise(*late)
             if g == 1:
-                short_cast(4, "scalar")
-            for gg in ((), (0, 1), (2, 3), ())[g]:
+                short_cast(5, "scalar")
+            for gg in PASSES[g]:
                 for i in range(4):
                     loss_product(i, 0, HALF, 4 + i, gg, gg + 1)
             if g == 2:
                 loss_out(0, 0, HALF)
                 loss_out(1, 0, HALF)
-                short_cast(5, "scalar")
                 loss_out(2, 0, HALF)
                 loss_out(3, 0, HALF)
         held = [6, 7, 2, 3, 5]
@@ -425,20 +432,22 @@ def tile_scenario_delta_gamma_losses_s7_kernel(
         turn_short(5, 0)
         short_quantise(4, 0, 2)
         short_quantise(4, 2, 4)
-        clip_tiles(3, range(4), 1)
+        clip_tiles(3, range(VQ_AT), 1)
+        v_quantise(2, 1)
+        clip_tiles(3, range(VQ_AT, 4), 1)
         for i in range(2, 4):
             loss_product(i, HALF, HALF, held[i], 0, 2)
         loss_product(4, 0, HALF, 4)
         loss_product(4, HALF, HALF, held[4], 0, 2)
-        short_cast(6, "scalar")
+        short_cast(6, W6)
         loss_out(4, 0, HALF)
         v_interleave(3, 1, "scalar", LATE_SHARE, HALF)
         short_scale_out(5, 0)
-        v_quantise(2, 1)
         short_scale_out(5, 1)
-        v_interleave(3, 1, "vector", 0, LATE_SHARE)
+        if LATE_SHARE:
+            v_interleave(3, 1, "vector", 0, LATE_SHARE)
         short_quantise(5)
-        short_cast(7, "vector")
+        short_cast(7, W7)
         for i in range(5):
             loss_product(i, HALF, HALF, held[i], 2, 3)
         turn_short(6, 0)
@@ -462,7 +471,5 @@ def tile_scenario_delta_gamma_losses_s7_kernel(
             loss_out(6, h * HALF, HALF)
         last = [(0, HALF), (HALF, HALF // 2), (3 * HALF // 2, HALF // 2)]
         for n, (c0, width) in enumerate(last):
-            loss_product(7, c0, width, (5, 0, 1)[n], 0, 2)
-        for n, (c0, width) in enumerate(last):
-            loss_product(7, c0, width, (5, 0, 1)[n], 2, 4)
+            loss_product(7, c0, width, (5, 0, 1)[n])
             loss_out(7, c0, width, "vector" if n == 1 else "scalar")

@@ -22,24 +22,16 @@ F_PASSES = F // K_PASS
 GROUPS = N // K_PASS
 HALF = S // 2
 BOOK_TILES = B // P
+PAIRS = 2 * GROUPS
 
 GROUPED_BUFS = 3
 TURNED_BUFS = 3
 SQUARES_BUFS = 6
 V_ROWS_BUFS = 5
 WIDE_BUFS = 4
-SHORT_BUFS = 8
 LOSS_BUFS = 4
-HEAD_SHARE = 320
-W3 = "scalar"
-W3_AT = 6
-I_AT = 3
-W7 = "scalar"
-S_TURNS = (0,)
-LATE_SHARE = 0
-PASSES = ((), (0, 1), (2, 3), ())
-VQ_AT = 4
-W6 = "scalar"
+
+HEAD_SHARE = 384
 
 
 def tile_scenario_delta_gamma_losses_s7_kernel(
@@ -113,11 +105,14 @@ def tile_scenario_delta_gamma_losses_s7_kernel(
             else:
                 nc.scalar.copy(out=d, in_=s)
 
+        def grouped_tile():
+            return work.tile([P, HALF, PACK], BF16, name="grouped", align_bytes=64, bufs=GROUPED_BUFS)
+
         shocks_grouped = {}
 
         def shocks_interleave(q, h, engine, c0=0, c1=HALF):
             if (q, h) not in shocks_grouped:
-                shocks_grouped[(q, h)] = work.tile([P, HALF, PACK], BF16, name="grouped", align_bytes=64, bufs=GROUPED_BUFS)
+                shocks_grouped[(q, h)] = grouped_tile()
             interleave(engine, shocks_grouped[(q, h)][:], shocks_raw[(q, h)][:], c0, c1)
 
         def shocks_quantise(q, h):
@@ -150,7 +145,7 @@ def tile_scenario_delta_gamma_losses_s7_kernel(
         def sens_copy(g, t):
             if t % 2 == 0:
                 sens_grouped[(g, t // 2)] = work.tile(
-                    [P, 2, F_PASSES, P, PACK], BF16, name="turned", align_bytes=64, bufs=TURNED_BUFS
+                    [P, 2, F_PASSES, P, PACK], BF16, name="sens_grouped", align_bytes=64, bufs=TURNED_BUFS
                 )
             copy_words_out(sens_grouped[(g, t // 2)][:, t % 2], sens_bank[(g, t)][:])
 
@@ -204,10 +199,9 @@ def tile_scenario_delta_gamma_losses_s7_kernel(
                 op1=ALU.min,
             )
 
-        def v_interleave(g, h, engine, c0=0, c1=HALF):
-            if (g, h) not in v_grouped:
-                v_grouped[(g, h)] = work.tile([P, HALF, PACK], BF16, name="grouped", align_bytes=64, bufs=GROUPED_BUFS)
-            interleave(engine, v_grouped[(g, h)][:], v_rows[(g, h)][:], c0, c1)
+        def v_interleave(g, h, engine):
+            v_grouped[(g, h)] = grouped_tile()
+            interleave(engine, v_grouped[(g, h)][:], v_rows[(g, h)][:], 0, HALF)
 
         def v_quantise(g, h):
             nc.vector.quantize_mx(
@@ -222,32 +216,33 @@ def tile_scenario_delta_gamma_losses_s7_kernel(
         short_grouped = {}
         short_operand = {}
 
-        def short_cast(i, engine, two0=0, two1=2):
+        def short_cast(i, engine="scalar", two0=0, two1=2):
             if i not in short_wide:
                 short_wide[i] = work.tile([P, 2, 2 * K_PASS], BF16, name="short_wide", bufs=WIDE_BUFS)
             codes = bytes_rows[i].bitcast(FP8)
+            dst = short_wide[i][:, two0:two1, :].rearrange("p a k -> p (a k)")
+            src = codes[:, 2 * two0 * K_PASS : 2 * two1 * K_PASS]
             if engine == "vector":
-                for two in range(two0, two1):
-                    nc.vector.tensor_scalar(
-                        out=short_wide[i][:, two, :].rearrange("p (u m e) -> p m u e", u=2, e=2),
-                        in0=codes[:, 2 * two * K_PASS : 2 * (two + 1) * K_PASS].rearrange("p (m u e) -> p m u e", u=2, e=2),
-                        scalar1=one[:],
-                        scalar2=None,
-                        op0=ALU.mult,
-                    )
-                    short_ordered.add((i, two))
+                nc.vector.tensor_copy(out=dst, in_=src)
             else:
-                nc.scalar.copy(
-                    out=short_wide[i][:, two0:two1, :].rearrange("p a k -> p (a k)"),
-                    in_=codes[:, 2 * two0 * K_PASS : 2 * two1 * K_PASS],
-                )
+                nc.scalar.copy(out=dst, in_=src)
+
+        def short_order(i):
+            words = short_wide[i][:].rearrange("p a k -> p (a k)").bitcast(F32)
+            short_wide[i] = work.tile([P, 2, 2 * K_PASS], BF16, name="short_words")
+            ordered = short_wide[i][:].rearrange("p a k -> p (a k)").bitcast(F32)
+            nc.vector.tensor_copy(
+                out=ordered.rearrange("p (a u m) -> p a u m", a=2, u=2),
+                in_=words.rearrange("p (a m u) -> p a u m", a=2, u=2),
+            )
+            short_ordered.add(i)
 
         def short_transpose(i, two, bank):
             short_bank[(i, two)] = psum.tile([P, 2, 2, P], F32, name="bank_%d" % bank)
             words = short_wide[i][:, two, :].bitcast(F32)
             for q in range(2):
                 for u in range(2):
-                    if (i, two) in short_ordered:
+                    if i in short_ordered:
                         piece = words[:, 256 * u + P * q : 256 * u + P * (q + 1)]
                     else:
                         piece = words[:, 256 * q + u : 256 * (q + 1) : 2]
@@ -268,8 +263,8 @@ def tile_scenario_delta_gamma_losses_s7_kernel(
 
         def short_quantise(i, g0=0, g1=GROUPS):
             if i not in short_operand:
-                codes = work.tile([P, GROUPS, P], U32, name="short_codes", align_bytes=64, bufs=SHORT_BUFS)
-                scales = work.tile([P, GROUPS, P], U8, name="short_scales", align_bytes=64, bufs=SHORT_BUFS)
+                codes = work.tile([P, GROUPS, P], U32, name="short_codes", align_bytes=64, bufs=BOOK_TILES)
+                scales = work.tile([P, GROUPS, P], U8, name="short_scales", align_bytes=64, bufs=BOOK_TILES)
                 short_operand[i] = (codes, scales)
             codes, scales = short_operand[i]
             nc.vector.quantize_mx(
@@ -304,20 +299,46 @@ def tile_scenario_delta_gamma_losses_s7_kernel(
                 nc.scalar.copy(out=rows[:], in_=loss_bank[(i, c0)][:])
             nc.sync.dma_start(out=out[i * P : (i + 1) * P, c0 : c0 + width], in_=rows[:])
 
-
-        one = keep.tile([P, 1], F32, name="one")
-        nc.vector.memset(one[:], 1.0)
         ident = keep.tile([P, P], F32, name="ident")
         make_identity(nc, ident[:])
+
+        def turn_sens(g, pair, bank):
+            for n in range(2):
+                sens_transpose(g, 2 * pair + n, bank + n)
+                sens_copy(g, 2 * pair + n)
+
+        def turn_short(i, bank):
+            for two in range(2):
+                short_transpose(i, two, bank + two)
+
+        def short_scale_out_both(i):
+            for two in range(2):
+                short_scale_out(i, two)
+
+        def short_quantise_halves(i):
+            short_quantise(i, 0, 2)
+            short_quantise(i, 2, 4)
+
+        def y_tiles(g, tiles, h, bank):
+            for n, t in enumerate(tiles):
+                y_product(g, t, h, bank + n)
+                y_square(g, t, h)
+
+        def clip_tiles(g, tiles, h):
+            for t in tiles:
+                v_clip(g, t, h)
+
+        def follow_v(tiles, h, banks, g0, g1):
+            for i in tiles:
+                loss_product(i, h * HALF, HALF, banks[i], g0, g1)
 
         load_scale()
         load_row_constants()
         load_bytes(0, 1)
         load_bytes(1, 1)
-        load_shocks(0, 0)
-        load_sens(0, 0, 2)
-        load_shocks(1, 0)
-        load_sens(0, 2, 2)
+        for q in range(F_PASSES):
+            load_shocks(q, 0)
+            load_sens(0, 2 * q, 2)
         load_bytes(2, 1)
         load_sens(1, 0, 2)
         load_sens(1, 2, 2)
@@ -328,24 +349,6 @@ def tile_scenario_delta_gamma_losses_s7_kernel(
         load_shocks(1, 1)
         load_sens(3, 0, 4)
         load_bytes(4, 4)
-
-        def turn_sens(g, tiles, bank):
-            for n, t in enumerate(tiles):
-                sens_transpose(g, t, bank + n)
-                sens_copy(g, t)
-
-        def turn_short(i, bank):
-            for two in range(2):
-                short_transpose(i, two, bank + two)
-
-        def y_tiles(g, tiles, h, bank):
-            for n, t in enumerate(tiles):
-                y_product(g, t, h, bank + n)
-                y_square(g, t, h)
-
-        def clip_tiles(g, tiles, h):
-            for t in tiles:
-                v_clip(g, t, h)
 
         for i in range(2):
             short_cast(i, "vector", 0, 1)
@@ -358,118 +361,118 @@ def tile_scenario_delta_gamma_losses_s7_kernel(
         shocks_interleave(0, 0, "scalar")
         short_scale_out(0, 0)
         short_scale_out(1, 0)
-        turn_sens(0, (0, 1), 4)
+        turn_sens(0, 0, 4)
         short_scale_out(0, 1)
         shocks_interleave(1, 0, "vector", 0, HEAD_SHARE)
         shocks_interleave(1, 0, "scalar", HEAD_SHARE, HALF)
         shocks_quantise(0, 0)
         sens_quantise(0, 0)
         shocks_quantise(1, 0)
-        turn_sens(0, (2, 3), 6)
-        short_cast(2, "scalar")
+        turn_sens(0, 1, 6)
+        short_cast(2)
         short_scale_out(1, 1)
         sens_quantise(0, 1)
         short_quantise(0)
-        for u in range(8):
-            g, pair = divmod(u, 2)
+
+        spare = [(shocks_interleave, shocks_quantise, 0, 1), (shocks_interleave, shocks_quantise, 1, 1)]
+        spare = spare + [(v_interleave, v_quantise, 0, 0), (v_interleave, v_quantise, 1, 0)]
+        spare_turn = [0, 2, 3, 5]
+        for n in range(PAIRS):
+            g, pair = divmod(n, 2)
             tiles = (2 * pair, 2 * pair + 1)
-            y_tiles(g, tiles, 0, 2 * (u % 2))
-            if u + 2 < 8:
-                turn_sens(g + 1, tiles, 4 + 2 * pair)
+            more_sens = g + 1 < GROUPS
+            y_tiles(g, tiles, 0, 2 * pair)
+            if more_sens:
+                turn_sens(g + 1, pair, 4 + 2 * pair)
             else:
-                turn_short(u - 4, 4 + 2 * pair)
-            if u == 0:
+                turn_short(2 + pair, 4 + 2 * pair)
+            if n == 0:
                 short_quantise(1)
-            if u in (0, 2):
-                shocks_interleave(u // 2, 1, "vector")
-            if u in (1, 3):
-                shocks_quantise(u // 2, 1)
-            if u == W3_AT:
-                short_cast(3, W3)
-            if u in (I_AT, I_AT + 2):
-                v_interleave((u - I_AT) // 2, 0, "vector")
-            if u in (I_AT + 1, I_AT + 3):
-                v_quantise((u - I_AT) // 2, 0)
+            if n == PAIRS // 2:
+                short_order(2)
+            for (copy, quantise, x, h), turn in zip(spare, spare_turn):
+                if n == turn:
+                    copy(x, h, "vector")
+                if n == turn + 1:
+                    quantise(x, h)
+            if n == PAIRS - 2:
+                short_cast(3)
             clip_tiles(g, tiles, 0)
-            if u + 2 < 8:
+            if more_sens:
                 sens_quantise(g + 1, pair)
             else:
-                if u == 7:
+                if pair == 1:
                     short_quantise(2)
-                short_scale_out(u - 4, 0)
-                short_scale_out(u - 4, 1)
-        short_cast(4, "scalar")
-        short_quantise(3)
-        for g in range(GROUPS):
-            y_tiles(g, range(4), 1, 0)
-            late = (g + 2, 0) if g + 2 < GROUPS else (g - 2, 1)
-            v_interleave(*late, "scalar" if g in S_TURNS else "vector")
-            if g < 3:
+                short_scale_out_both(2 + pair)
+        short_cast(4)
+        short_quantise_halves(3)
+
+        first_tiles = range(4)
+        for g in range(GROUPS - 1):
+            y_tiles(g, range(PACK), 1, 0)
+            behind = (g + 2, 0) if g + 2 < GROUPS else (g - 2, 1)
+            if g == 0:
+                v_interleave(*behind, "scalar")
+                clip_tiles(g, range(PACK), 1)
+                short_order(4)
+                v_quantise(*behind)
+            else:
+                v_interleave(*behind, "vector")
                 clip_tiles(g, (0, 1), 1)
-            if g not in S_TURNS or g == 3:
-                v_quantise(*late)
-            if g < 3:
+                v_quantise(*behind)
                 clip_tiles(g, (2, 3), 1)
-            if g in S_TURNS and g < 3:
-                v_quantise(*late)
-            if g == 1:
-                short_cast(5, "scalar")
-            for gg in PASSES[g]:
-                for i in range(4):
-                    loss_product(i, 0, HALF, 4 + i, gg, gg + 1)
-            if g == 2:
-                loss_out(0, 0, HALF)
-                loss_out(1, 0, HALF)
-                loss_out(2, 0, HALF)
-                loss_out(3, 0, HALF)
+                if g == 1:
+                    short_cast(5)
+                for passed in (2 * g - 2, 2 * g - 1):
+                    follow_v(first_tiles, 0, [4, 5, 6, 7], passed, passed + 1)
+        for i in first_tiles:
+            loss_out(i, 0, HALF)
+        y_tiles(GROUPS - 1, range(PACK), 1, 0)
+        v_interleave(1, 1, "vector")
+        v_quantise(1, 1)
+
         held = [6, 7, 2, 3, 5]
         turn_short(4, 4)
-        short_scale_out(4, 0)
-        short_scale_out(4, 1)
+        short_scale_out_both(4)
         v_interleave(2, 1, "scalar")
-        for i in range(2):
-            loss_product(i, HALF, HALF, held[i], 0, 2)
+        follow_v((0, 1), 1, held, 0, 2)
         turn_short(5, 0)
-        short_quantise(4, 0, 2)
-        short_quantise(4, 2, 4)
-        clip_tiles(3, range(VQ_AT), 1)
+        short_quantise_halves(4)
+        clip_tiles(GROUPS - 1, range(PACK), 1)
         v_quantise(2, 1)
-        clip_tiles(3, range(VQ_AT, 4), 1)
-        for i in range(2, 4):
-            loss_product(i, HALF, HALF, held[i], 0, 2)
+        follow_v((2, 3), 1, held, 0, 2)
         loss_product(4, 0, HALF, 4)
-        loss_product(4, HALF, HALF, held[4], 0, 2)
-        short_cast(6, W6)
+        follow_v((4,), 1, held, 0, 2)
+        short_cast(6)
         loss_out(4, 0, HALF)
-        v_interleave(3, 1, "scalar", LATE_SHARE, HALF)
-        short_scale_out(5, 0)
-        short_scale_out(5, 1)
-        if LATE_SHARE:
-            v_interleave(3, 1, "vector", 0, LATE_SHARE)
-        short_quantise(5)
-        short_cast(7, W7)
-        for i in range(5):
-            loss_product(i, HALF, HALF, held[i], 2, 3)
+        v_interleave(3, 1, "scalar")
+        short_scale_out_both(5)
+        short_quantise_halves(5)
+        short_cast(7)
+        follow_v(range(5), 1, held, 2, 3)
         turn_short(6, 0)
         loss_product(5, 0, HALF, 4)
         loss_out(5, 0, HALF)
         v_quantise(3, 1)
+        short_scale_out(6, 0)
+        short_order(7)
+        short_scale_out(6, 1)
         for i in range(5):
-            loss_product(i, HALF, HALF, held[i], 3, 4)
+            follow_v((i,), 1, held, 3, 4)
             loss_out(i, HALF, HALF)
         short_transpose(7, 0, 4)
         short_transpose(7, 1, 6)
-        for i in (6, 7):
-            short_scale_out(i, 0)
-            short_scale_out(i, 1)
-            short_quantise(i, 0, 2)
-            short_quantise(i, 2, 4)
+        short_quantise_halves(6)
+        short_scale_out_both(7)
+        short_quantise_halves(7)
         loss_product(5, HALF, HALF, 7)
         loss_out(5, HALF, HALF)
         for h in range(2):
             loss_product(6, h * HALF, HALF, 2 + h)
             loss_out(6, h * HALF, HALF)
-        last = [(0, HALF), (HALF, HALF // 2), (3 * HALF // 2, HALF // 2)]
-        for n, (c0, width) in enumerate(last):
-            loss_product(7, c0, width, (5, 0, 1)[n])
-            loss_out(7, c0, width, "vector" if n == 1 else "scalar")
+        quarter = HALF // 2
+        for c0, width, bank, engine in (
+            (0, HALF, 5, "scalar"), (HALF, quarter, 0, "vector"), (HALF + quarter, quarter, 1, "scalar")
+        ):
+            loss_product(7, c0, width, bank)
+            loss_out(7, c0, width, engine)

@@ -79,18 +79,21 @@ def tile_scenario_delta_gamma_losses_s7_kernel(
                 out=scale_sb[:, :, 0:PACK], in_=short_scale.rearrange("o (g p t) -> p (o g) t", p=P, t=PACK)
             )
 
-        def load_row_constants():
-            nc.scalar.dma_start(out=tilt_raw[:, :, 0:PACK], in_=tilt.rearrange("(g m t) -> m g t", m=P, t=PACK))
-            nc.scalar.dma_start(out=cap_raw[:, :, 0:PACK], in_=cap.rearrange("(g m t) -> m g t", m=P, t=PACK))
+        def load_row_constants(queue, g0, g1):
+            for raw, vector in ((tilt_raw, tilt), (cap_raw, cap)):
+                queue.dma_start(
+                    out=raw[:, g0:g1, 0:PACK], in_=vector.rearrange("(g m t) -> m g t", m=P, t=PACK)[:, g0:g1, :]
+                )
 
         half_tilt = keep.tile([P, GROUPS, PACK], F32, name="half_tilt")
         half_tilt_sq = keep.tile([P, GROUPS, PACK], F32, name="half_tilt_sq")
         cap_f32 = keep.tile([P, GROUPS, PACK], F32, name="cap_f32")
 
-        def row_constants():
-            nc.scalar.activation(out=half_tilt[:], in_=tilt_raw[:, :, 0:PACK], func=ACT.Copy, scale=0.5)
-            nc.scalar.activation(out=half_tilt_sq[:], in_=tilt_raw[:, :, 0:PACK], func=ACT.Square, scale=0.5)
-            nc.scalar.copy(out=cap_f32[:], in_=cap_raw[:, :, 0:PACK])
+        def row_constants(g0, g1):
+            raw = tilt_raw[:, g0:g1, 0:PACK]
+            nc.scalar.activation(out=half_tilt[:, g0:g1], in_=raw, func=ACT.Copy, scale=0.5)
+            nc.scalar.activation(out=half_tilt_sq[:, g0:g1], in_=raw, func=ACT.Square, scale=0.5)
+            nc.scalar.copy(out=cap_f32[:, g0:g1], in_=cap_raw[:, g0:g1, 0:PACK])
 
         shocks_codes = keep.tile([P, F_PASSES, S], U32, name="shocks_codes", align_bytes=64)
         shocks_scales = keep.tile([P, F_PASSES, S], U8, name="shocks_scales", align_bytes=64)
@@ -333,20 +336,21 @@ def tile_scenario_delta_gamma_losses_s7_kernel(
                 loss_product(i, h * HALF, HALF, banks[i], g0, g1)
 
         load_scale()
-        load_row_constants()
+        load_row_constants(nc.scalar, 0, 1)
         load_bytes(0, 1)
         load_bytes(1, 1)
         for q in range(F_PASSES):
             load_shocks(q, 0)
             load_sens(0, 2 * q, 2)
-        load_bytes(2, 1)
         load_sens(1, 0, 2)
+        load_bytes(2, 1)
         load_sens(1, 2, 2)
-        load_bytes(3, 1)
         load_shocks(0, 1)
         load_sens(2, 0, 2)
+        load_row_constants(nc.sync, 1, GROUPS)
         load_sens(2, 2, 2)
         load_shocks(1, 1)
+        load_bytes(3, 1)
         load_sens(3, 0, 4)
         load_bytes(4, 4)
 
@@ -357,7 +361,7 @@ def tile_scenario_delta_gamma_losses_s7_kernel(
         short_transpose(1, 0, 1)
         short_transpose(0, 1, 2)
         short_transpose(1, 1, 3)
-        row_constants()
+        row_constants(0, 1)
         shocks_interleave(0, 0, "scalar")
         short_scale_out(0, 0)
         short_scale_out(1, 0)
@@ -381,6 +385,8 @@ def tile_scenario_delta_gamma_losses_s7_kernel(
             g, pair = divmod(n, 2)
             tiles = (2 * pair, 2 * pair + 1)
             more_sens = g + 1 < GROUPS
+            if n == 2:
+                row_constants(1, GROUPS)
             y_tiles(g, tiles, 0, 2 * pair)
             if more_sens:
                 turn_sens(g + 1, pair, 4 + 2 * pair)

@@ -29,9 +29,9 @@ TURNED_BUFS = 3
 SQUARES_BUFS = 6
 V_ROWS_BUFS = 5
 WIDE_BUFS = 4
-LOSS_BUFS = 4
 
 HEAD_SHARE = 384
+POOL_SHARE = 384
 
 
 def tile_scenario_delta_gamma_losses_s7_kernel(
@@ -206,6 +206,18 @@ def tile_scenario_delta_gamma_losses_s7_kernel(
             v_grouped[(g, h)] = grouped_tile()
             interleave(engine, v_grouped[(g, h)][:], v_rows[(g, h)][:], 0, HALF)
 
+        def v_interleave_shared(g, h):
+            v_grouped[(g, h)] = grouped_tile()
+            nc.gpsimd.tensor_scalar(
+                out=v_grouped[(g, h)][:, 0:POOL_SHARE, :],
+                in0=v_rows[(g, h)][:, :, 0:POOL_SHARE].rearrange("p t n -> p n t"),
+                scalar1=1.0,
+                scalar2=0.0,
+                op0=ALU.mult,
+                op1=ALU.add,
+            )
+            interleave("scalar", v_grouped[(g, h)][:], v_rows[(g, h)][:], POOL_SHARE, HALF)
+
         def v_quantise(g, h):
             nc.vector.quantize_mx(
                 out=v_codes[g][:, half_cols(h)].bitcast(FP8X4),
@@ -277,6 +289,10 @@ def tile_scenario_delta_gamma_losses_s7_kernel(
             )
 
         loss_bank = {}
+        stage = []
+        staged = []
+        spent = ["sens_rows_%d_%d" % (g, t0) for g in range(3) for t0 in (0, 2)]
+        spent = spent + ["shocks_raw_%d_%d" % (q, h) for h in range(2) for q in range(2)]
 
         def loss_product(i, c0, width, bank, g0=0, g1=GROUPS):
             codes, scales = short_operand[i]
@@ -295,12 +311,16 @@ def tile_scenario_delta_gamma_losses_s7_kernel(
                 )
 
         def loss_out(i, c0, width, engine="scalar"):
-            rows = work.tile([P, width], F32, name="loss_rows", bufs=LOSS_BUFS)
+            n = len(staged)
+            if n % 2 == 0:
+                stage.append(keep.tile([P, 2, HALF], F32, name=spent[n // 2]))
+            rows = stage[-1][:, n % 2, 0:width]
+            staged.append((i, c0))
             if engine == "vector":
-                nc.vector.tensor_copy(out=rows[:], in_=loss_bank[(i, c0)][:])
+                nc.vector.tensor_copy(out=rows, in_=loss_bank[(i, c0)][:])
             else:
-                nc.scalar.copy(out=rows[:], in_=loss_bank[(i, c0)][:])
-            nc.sync.dma_start(out=out[i * P : (i + 1) * P, c0 : c0 + width], in_=rows[:])
+                nc.scalar.copy(out=rows, in_=loss_bank[(i, c0)][:])
+            nc.sync.dma_start(out=out[i * P : (i + 1) * P, c0 : c0 + width], in_=rows)
 
         ident = keep.tile([P, P], F32, name="ident")
         make_identity(nc, ident[:])
@@ -411,6 +431,7 @@ def tile_scenario_delta_gamma_losses_s7_kernel(
                     short_quantise(2)
                 short_scale_out_both(2 + pair)
         short_cast(4)
+        v_interleave_shared(3, 0)
         short_quantise_halves(3)
 
         first_tiles = range(4)
@@ -418,14 +439,17 @@ def tile_scenario_delta_gamma_losses_s7_kernel(
             y_tiles(g, range(PACK), 1, 0)
             behind = (g + 2, 0) if g + 2 < GROUPS else (g - 2, 1)
             if g == 0:
-                v_interleave(*behind, "scalar")
+                v_interleave(*behind, "vector")
                 clip_tiles(g, range(PACK), 1)
                 short_order(4)
                 v_quantise(*behind)
             else:
-                v_interleave(*behind, "vector")
+                if g == 2:
+                    v_interleave(*behind, "vector")
                 clip_tiles(g, (0, 1), 1)
                 v_quantise(*behind)
+                if g == 2:
+                    v_interleave(1, 1, "vector")
                 clip_tiles(g, (2, 3), 1)
                 if g == 1:
                     short_cast(5)
@@ -434,13 +458,12 @@ def tile_scenario_delta_gamma_losses_s7_kernel(
         for i in first_tiles:
             loss_out(i, 0, HALF)
         y_tiles(GROUPS - 1, range(PACK), 1, 0)
-        v_interleave(1, 1, "vector")
         v_quantise(1, 1)
 
         held = [6, 7, 2, 3, 5]
         turn_short(4, 4)
         short_scale_out_both(4)
-        v_interleave(2, 1, "scalar")
+        v_interleave_shared(2, 1)
         follow_v((0, 1), 1, held, 0, 2)
         turn_short(5, 0)
         short_quantise_halves(4)
@@ -451,7 +474,7 @@ def tile_scenario_delta_gamma_losses_s7_kernel(
         follow_v((4,), 1, held, 0, 2)
         short_cast(6)
         loss_out(4, 0, HALF)
-        v_interleave(3, 1, "scalar")
+        v_interleave_shared(3, 1)
         short_scale_out_both(5)
         short_quantise_halves(5)
         short_cast(7)

@@ -24,14 +24,16 @@ HALF = S // 2
 BOOK_TILES = B // P
 PAIRS = 2 * GROUPS
 
-GROUPED_BUFS = 3
+GROUPED_BUFS = 4
 TURNED_BUFS = 3
 SQUARES_BUFS = 6
 V_ROWS_BUFS = 5
-WIDE_BUFS = 4
+WIDE_BUFS = 3
+SCALED_BUFS = 2
+ORDERED_BUFS = 3
 
-HEAD_SHARE = 384
-POOL_SHARE = 384
+HEAD_SHARE = 128
+POOL_SHARE = 320
 
 
 def tile_scenario_delta_gamma_losses_s7_kernel(
@@ -48,6 +50,7 @@ def tile_scenario_delta_gamma_losses_s7_kernel(
         shocks_view = shocks.rearrange("(g p t) s -> g p t s", p=P, t=PACK)
         bytes_view = short_bytes.rearrange("(i p) k -> p i k", p=P)
         sens_rows = {}
+        sens_pairs = {}
         shocks_raw = {}
         bytes_rows = {}
         scale_sb = keep.tile([P, GROUPS, 8], F32, name="scale_sb")
@@ -57,11 +60,12 @@ def tile_scenario_delta_gamma_losses_s7_kernel(
         def half_cols(h):
             return slice(h * HALF, (h + 1) * HALF)
 
-        def load_sens(g, t0, n):
-            rows = keep.tile([P, n, F], BF16, name="sens_rows_%d_%d" % (g, t0))
-            nc.sync.dma_start(out=rows[:], in_=sens_view[g][:, t0 : t0 + n, :])
-            for t in range(n):
-                sens_rows[(g, t0 + t)] = rows[:, t, :]
+        def load_sens(g, pair):
+            rows = keep.tile([P, 2, F], BF16, name="sens_rows_%d_%d" % (g, pair))
+            nc.sync.dma_start(out=rows[:], in_=sens_view[g][:, 2 * pair : 2 * pair + 2, :])
+            sens_pairs[(g, pair)] = rows[:].rearrange("p a k -> p (a k)")
+            for n in range(2):
+                sens_rows[(g, 2 * pair + n)] = rows[:, n, :]
 
         def load_shocks(q, h):
             raw = keep.tile([P, PACK, HALF], BF16, name="shocks_raw_%d_%d" % (q, h))
@@ -72,7 +76,14 @@ def tile_scenario_delta_gamma_losses_s7_kernel(
             rows = keep.tile([P, n, N], U8, name="bytes_rows_%d" % i0)
             nc.sync.dma_start(out=rows[:], in_=bytes_view[:, i0 : i0 + n, :])
             for i in range(n):
+                for two in range(2):
+                    bytes_rows[(i0 + i, two)] = rows[:, i, 2 * two * K_PASS : 2 * (two + 1) * K_PASS]
                 bytes_rows[i0 + i] = rows[:, i, :]
+
+        def load_bytes_half(i, two):
+            rows = keep.tile([P, 2 * K_PASS], U8, name="bytes_half_%d_%d" % (i, two))
+            nc.sync.dma_start(out=rows[:], in_=bytes_view[:, i, 2 * two * K_PASS : 2 * (two + 1) * K_PASS])
+            bytes_rows[(i, two)] = rows[:]
 
         def load_scale():
             nc.scalar.dma_start(
@@ -105,8 +116,17 @@ def tile_scenario_delta_gamma_losses_s7_kernel(
             s = src.rearrange("p t (b c) -> p b t c", c=4)[:, c0 // 4 : c1 // 4]
             if engine == "vector":
                 nc.vector.tensor_copy(out=d, in_=s)
-            else:
+            elif engine == "scalar":
                 nc.scalar.copy(out=d, in_=s)
+            else:
+                nc.gpsimd.tensor_scalar(
+                    out=dst[:, c0:c1, :],
+                    in0=src[:, :, c0:c1].rearrange("p t n -> p n t"),
+                    scalar1=1.0,
+                    scalar2=0.0,
+                    op0=ALU.mult,
+                    op1=ALU.add,
+                )
 
         def grouped_tile():
             return work.tile([P, HALF, PACK], BF16, name="grouped", align_bytes=64, bufs=GROUPED_BUFS)
@@ -135,15 +155,33 @@ def tile_scenario_delta_gamma_losses_s7_kernel(
         sens_bank = {}
         sens_grouped = {}
         sens_operand = {}
+        sens_ordered = set()
 
         def sens_transpose(g, t, bank):
             sens_bank[(g, t)] = psum.tile([P, F_PASSES, 2, P], F32, name="bank_%d" % bank)
             words = sens_rows[(g, t)].bitcast(F32)
             for q in range(F_PASSES):
                 for u in range(2):
-                    nc.tensor.transpose(
-                        sens_bank[(g, t)][:, q, u, :], words[:, 256 * q + u : 256 * (q + 1) : 2], ident[:]
-                    )
+                    if (g, t // 2) in sens_ordered:
+                        piece = words[:, 256 * u + P * q : 256 * u + P * (q + 1)]
+                    else:
+                        piece = words[:, 256 * q + u : 256 * (q + 1) : 2]
+                    nc.tensor.transpose(sens_bank[(g, t)][:, q, u, :], piece, ident[:])
+
+        def order_words(engine, dst, src):
+            d = dst.bitcast(F32).rearrange("p (a u m) -> p a u m", a=2, u=2)
+            s = src.bitcast(F32).rearrange("p (a m u) -> p a u m", a=2, u=2)
+            if engine == "vector":
+                nc.vector.tensor_copy(out=d, in_=s)
+            else:
+                nc.scalar.copy(out=d, in_=s)
+
+        def sens_order(g, pair, engine="vector"):
+            ordered = work.tile([P, 2, F], BF16, name="ordered", bufs=ORDERED_BUFS)
+            order_words(engine, ordered[:].rearrange("p a k -> p (a k)"), sens_pairs[(g, pair)])
+            for n in range(2):
+                sens_rows[(g, 2 * pair + n)] = ordered[:, n, :]
+            sens_ordered.add((g, pair))
 
         def sens_copy(g, t):
             if t % 2 == 0:
@@ -152,15 +190,17 @@ def tile_scenario_delta_gamma_losses_s7_kernel(
                 )
             copy_words_out(sens_grouped[(g, t // 2)][:, t % 2], sens_bank[(g, t)][:])
 
-        def sens_quantise(g, pair):
-            codes = keep.tile([P, 2, F_PASSES, P], U32, name="sens_codes_%d_%d" % (g, pair), align_bytes=64)
-            scales = keep.tile([P, 2, F_PASSES, P], U8, name="sens_scales_%d_%d" % (g, pair), align_bytes=64)
+        def sens_quantise(g, pair, a0=0, a1=2):
+            if (g, pair) not in sens_operand:
+                codes = keep.tile([P, 2, F_PASSES, P], U32, name="sens_codes_%d_%d" % (g, pair), align_bytes=64)
+                scales = keep.tile([P, 2, F_PASSES, P], U8, name="sens_scales_%d_%d" % (g, pair), align_bytes=64)
+                sens_operand[(g, pair)] = (codes, scales)
+            codes, scales = sens_operand[(g, pair)]
             nc.vector.quantize_mx(
-                out=codes[:].rearrange("p a q m -> p (a q m)").bitcast(FP8X4),
-                scales=scales[:].rearrange("p a q m -> p (a q m)"),
-                in_=sens_grouped[(g, pair)][:].rearrange("p a q m j -> p (a q m j)"),
+                out=codes[:, a0:a1].rearrange("p a q m -> p (a q m)").bitcast(FP8X4),
+                scales=scales[:, a0:a1].rearrange("p a q m -> p (a q m)"),
+                in_=sens_grouped[(g, pair)][:, a0:a1].rearrange("p a q m j -> p (a q m j)"),
             )
-            sens_operand[(g, pair)] = (codes, scales)
 
         y_bank = {}
         squares = {}
@@ -202,21 +242,10 @@ def tile_scenario_delta_gamma_losses_s7_kernel(
                 op1=ALU.min,
             )
 
-        def v_interleave(g, h, engine):
-            v_grouped[(g, h)] = grouped_tile()
-            interleave(engine, v_grouped[(g, h)][:], v_rows[(g, h)][:], 0, HALF)
-
-        def v_interleave_shared(g, h):
-            v_grouped[(g, h)] = grouped_tile()
-            nc.gpsimd.tensor_scalar(
-                out=v_grouped[(g, h)][:, 0:POOL_SHARE, :],
-                in0=v_rows[(g, h)][:, :, 0:POOL_SHARE].rearrange("p t n -> p n t"),
-                scalar1=1.0,
-                scalar2=0.0,
-                op0=ALU.mult,
-                op1=ALU.add,
-            )
-            interleave("scalar", v_grouped[(g, h)][:], v_rows[(g, h)][:], POOL_SHARE, HALF)
+        def v_interleave(g, h, engine, c0=0, c1=HALF):
+            if (g, h) not in v_grouped:
+                v_grouped[(g, h)] = grouped_tile()
+            interleave(engine, v_grouped[(g, h)][:], v_rows[(g, h)][:], c0, c1)
 
         def v_quantise(g, h):
             nc.vector.quantize_mx(
@@ -234,22 +263,17 @@ def tile_scenario_delta_gamma_losses_s7_kernel(
         def short_cast(i, engine="scalar", two0=0, two1=2):
             if i not in short_wide:
                 short_wide[i] = work.tile([P, 2, 2 * K_PASS], BF16, name="short_wide", bufs=WIDE_BUFS)
-            codes = bytes_rows[i].bitcast(FP8)
             dst = short_wide[i][:, two0:two1, :].rearrange("p a k -> p (a k)")
-            src = codes[:, 2 * two0 * K_PASS : 2 * two1 * K_PASS]
+            src = (bytes_rows[i] if two1 - two0 == 2 else bytes_rows[(i, two0)]).bitcast(FP8)
             if engine == "vector":
                 nc.vector.tensor_copy(out=dst, in_=src)
             else:
                 nc.scalar.copy(out=dst, in_=src)
 
-        def short_order(i):
-            words = short_wide[i][:].rearrange("p a k -> p (a k)").bitcast(F32)
-            short_wide[i] = work.tile([P, 2, 2 * K_PASS], BF16, name="short_words")
-            ordered = short_wide[i][:].rearrange("p a k -> p (a k)").bitcast(F32)
-            nc.vector.tensor_copy(
-                out=ordered.rearrange("p (a u m) -> p a u m", a=2, u=2),
-                in_=words.rearrange("p (a m u) -> p a u m", a=2, u=2),
-            )
+        def short_order(i, engine="vector"):
+            wide = short_wide[i][:].rearrange("p a k -> p (a k)")
+            short_wide[i] = work.tile([P, 2, 2 * K_PASS], BF16, name="ordered", bufs=ORDERED_BUFS)
+            order_words(engine, short_wide[i][:].rearrange("p a k -> p (a k)"), wide)
             short_ordered.add(i)
 
         def short_transpose(i, two, bank):
@@ -265,7 +289,7 @@ def tile_scenario_delta_gamma_losses_s7_kernel(
 
         def short_scale_out(i, two):
             if two == 0:
-                short_grouped[i] = work.tile([P, GROUPS, P, PACK], BF16, name="short_grouped", align_bytes=64)
+                short_grouped[i] = work.tile([P, GROUPS, P, PACK], BF16, name="short_grouped", align_bytes=64, bufs=SCALED_BUFS)
             passes = slice(2 * two, 2 * two + 2)
             values = short_bank[(i, two)][:].rearrange("p u q m -> p (u q m)").bitcast(BF16)
             factors = scale_sb[:, passes, 0:PACK].rearrange("p q (u e) -> p q u e", u=2)
@@ -291,7 +315,7 @@ def tile_scenario_delta_gamma_losses_s7_kernel(
         loss_bank = {}
         stage = []
         staged = []
-        spent = ["sens_rows_%d_%d" % (g, t0) for g in range(3) for t0 in (0, 2)]
+        spent = ["sens_rows_%d_%d" % (g, t0) for g in range(GROUPS) for t0 in range(2)]
         spent = spent + ["shocks_raw_%d_%d" % (q, h) for h in range(2) for q in range(2)]
 
         def loss_product(i, c0, width, bank, g0=0, g1=GROUPS):
@@ -310,7 +334,7 @@ def tile_scenario_delta_gamma_losses_s7_kernel(
                     stop=(g == GROUPS - 1),
                 )
 
-        def loss_out(i, c0, width, engine="scalar"):
+        def loss_out(i, c0, width, engine="scalar", queue=nc.sync):
             n = len(staged)
             if n % 2 == 0:
                 stage.append(keep.tile([P, 2, HALF], F32, name=spent[n // 2]))
@@ -320,7 +344,7 @@ def tile_scenario_delta_gamma_losses_s7_kernel(
                 nc.vector.tensor_copy(out=rows, in_=loss_bank[(i, c0)][:])
             else:
                 nc.scalar.copy(out=rows, in_=loss_bank[(i, c0)][:])
-            nc.sync.dma_start(out=out[i * P : (i + 1) * P, c0 : c0 + width], in_=rows)
+            queue.dma_start(out=out[i * P : (i + 1) * P, c0 : c0 + width], in_=rows)
 
         ident = keep.tile([P, P], F32, name="ident")
         make_identity(nc, ident[:])
@@ -356,42 +380,45 @@ def tile_scenario_delta_gamma_losses_s7_kernel(
                 loss_product(i, h * HALF, HALF, banks[i], g0, g1)
 
         load_scale()
-        load_row_constants(nc.scalar, 0, 1)
-        load_bytes(0, 1)
+        load_bytes_half(0, 0)
+        load_bytes_half(0, 1)
         load_bytes(1, 1)
         for q in range(F_PASSES):
             load_shocks(q, 0)
-            load_sens(0, 2 * q, 2)
-        load_sens(1, 0, 2)
+        load_sens(0, 0)
+        load_row_constants(nc.sync, 0, 1)
+        load_sens(0, 1)
+        load_sens(1, 0)
         load_bytes(2, 1)
-        load_sens(1, 2, 2)
+        load_sens(1, 1)
         load_shocks(0, 1)
-        load_sens(2, 0, 2)
+        load_sens(2, 0)
         load_row_constants(nc.sync, 1, GROUPS)
-        load_sens(2, 2, 2)
+        load_sens(2, 1)
         load_shocks(1, 1)
         load_bytes(3, 1)
-        load_sens(3, 0, 4)
+        load_sens(3, 0)
+        load_sens(3, 1)
         load_bytes(4, 4)
 
-        for i in range(2):
-            short_cast(i, "vector", 0, 1)
-            short_cast(i, "scalar", 1, 2)
-        short_transpose(0, 0, 0)
-        short_transpose(1, 0, 1)
-        short_transpose(0, 1, 2)
-        short_transpose(1, 1, 3)
-        row_constants(0, 1)
-        shocks_interleave(0, 0, "scalar")
-        short_scale_out(0, 0)
+        short_cast(0, "vector", 0, 1)
+        short_cast(0, "scalar", 1, 2)
+        for two in range(2):
+            short_cast(1, "scalar", two, two + 1)
+        turn_short(0, 0)
+        turn_short(1, 2)
+        shocks_interleave(0, 0, "gpsimd", 0, POOL_SHARE)
+        shocks_interleave(0, 0, "scalar", POOL_SHARE, HALF)
+        shocks_interleave(1, 0, "scalar", HEAD_SHARE, HALF)
+        short_scale_out_both(0)
         short_scale_out(1, 0)
         turn_sens(0, 0, 4)
-        short_scale_out(0, 1)
         shocks_interleave(1, 0, "vector", 0, HEAD_SHARE)
-        shocks_interleave(1, 0, "scalar", HEAD_SHARE, HALF)
         shocks_quantise(0, 0)
-        sens_quantise(0, 0)
         shocks_quantise(1, 0)
+        sens_quantise(0, 0, 0, 1)
+        sens_quantise(0, 0, 1, 2)
+        row_constants(0, 1)
         turn_sens(0, 1, 6)
         short_cast(2)
         short_scale_out(1, 1)
@@ -419,30 +446,45 @@ def tile_scenario_delta_gamma_losses_s7_kernel(
             for (copy, quantise, x, h), turn in zip(spare, spare_turn):
                 if n == turn:
                     copy(x, h, "vector")
-                if n == turn + 1:
+                if n == turn + 1 and n != PAIRS - 2:
                     quantise(x, h)
-            if n == PAIRS - 2:
-                short_cast(3)
-            clip_tiles(g, tiles, 0)
-            if more_sens:
+            if n in (3, 5):
+                short_cast(3, "scalar", n // 4, n // 4 + 1)
+            if n == PAIRS - 3:
+                clip_tiles(g, tiles[:1], 0)
                 sens_quantise(g + 1, pair)
+                short_order(3)
+            elif n == PAIRS - 2:
+                clip_tiles(g, tiles, 0)
+                clip_tiles(g - 1, (3,), 0)
+                v_quantise(1, 0)
+                v_interleave(2, 0, "gpsimd", 0, POOL_SHARE)
+            else:
+                clip_tiles(g, tiles, 0)
+            if more_sens:
+                if n != PAIRS - 3:
+                    sens_quantise(g + 1, pair)
             else:
                 if pair == 1:
                     short_quantise(2)
                 short_scale_out_both(2 + pair)
-        short_cast(4)
-        v_interleave_shared(3, 0)
+        v_interleave(3, 0, "gpsimd", 0, POOL_SHARE)
+        v_interleave(2, 0, "scalar", POOL_SHARE, HALF)
         short_quantise_halves(3)
 
         first_tiles = range(4)
         for g in range(GROUPS - 1):
-            y_tiles(g, range(PACK), 1, 0)
+            if g == 1:
+                y_tiles(g, (0, 1), 1, 0)
+                short_cast(4)
+                y_tiles(g, (2, 3), 1, 2)
+            else:
+                y_tiles(g, range(PACK), 1, 0)
             behind = (g + 2, 0) if g + 2 < GROUPS else (g - 2, 1)
             if g == 0:
-                v_interleave(*behind, "vector")
-                clip_tiles(g, range(PACK), 1)
-                short_order(4)
+                v_interleave(3, 0, "scalar", POOL_SHARE, HALF)
                 v_quantise(*behind)
+                clip_tiles(g, range(PACK), 1)
             else:
                 if g == 2:
                     v_interleave(*behind, "vector")
@@ -450,42 +492,48 @@ def tile_scenario_delta_gamma_losses_s7_kernel(
                 v_quantise(*behind)
                 if g == 2:
                     v_interleave(1, 1, "vector")
-                clip_tiles(g, (2, 3), 1)
+                clip_tiles(g, (2, 3) if g == 1 else (2,), 1)
                 if g == 1:
-                    short_cast(5)
-                for passed in (2 * g - 2, 2 * g - 1):
-                    follow_v(first_tiles, 0, [4, 5, 6, 7], passed, passed + 1)
+                    short_order(4, "scalar")
+                follow_v(first_tiles, 0, [4, 5, 6, 7], 2 * g - 2, 2 * g)
+        short_cast(5)
         for i in first_tiles:
             loss_out(i, 0, HALF)
-        y_tiles(GROUPS - 1, range(PACK), 1, 0)
+        short_order(5)
+        clip_tiles(2, (3,), 1)
         v_quantise(1, 1)
+        v_interleave(2, 1, "gpsimd", 0, POOL_SHARE)
+        y_tiles(GROUPS - 1, range(PACK), 1, 0)
 
         held = [6, 7, 2, 3, 5]
         turn_short(4, 4)
         short_scale_out_both(4)
-        v_interleave_shared(2, 1)
+        short_cast(6)
+        short_order(6, "scalar")
         follow_v((0, 1), 1, held, 0, 2)
         turn_short(5, 0)
-        short_quantise_halves(4)
+        short_quantise(4, 0, 2)
+        v_interleave(2, 1, "vector", POOL_SHARE, HALF)
+        short_quantise(4, 2, 4)
         clip_tiles(GROUPS - 1, range(PACK), 1)
         v_quantise(2, 1)
         follow_v((2, 3), 1, held, 0, 2)
         loss_product(4, 0, HALF, 4)
         follow_v((4,), 1, held, 0, 2)
-        short_cast(6)
+        v_interleave(3, 1, "gpsimd", 0, POOL_SHARE)
         loss_out(4, 0, HALF)
-        v_interleave_shared(3, 1)
         short_scale_out_both(5)
-        short_quantise_halves(5)
+        short_quantise(5, 0, 2)
+        v_interleave(3, 1, "vector", POOL_SHARE, HALF)
+        short_quantise(5, 2, 4)
         short_cast(7)
+        short_order(7, "scalar")
         follow_v(range(5), 1, held, 2, 3)
         turn_short(6, 0)
         loss_product(5, 0, HALF, 4)
         loss_out(5, 0, HALF)
         v_quantise(3, 1)
-        short_scale_out(6, 0)
-        short_order(7)
-        short_scale_out(6, 1)
+        short_scale_out_both(6)
         for i in range(5):
             follow_v((i,), 1, held, 3, 4)
             loss_out(i, HALF, HALF)

@@ -26,13 +26,13 @@ PAIRS = 2 * GROUPS
 
 GROUPED_BUFS = 4
 TURNED_BUFS = 3
-SQUARES_BUFS = 6
+SQUARES_BUFS = 7
 V_ROWS_BUFS = 5
 WIDE_BUFS = 3
 SCALED_BUFS = 2
 ORDERED_BUFS = 3
 
-HEAD_SHARE = 128
+HEAD_SHARE = 224
 POOL_SHARE = 320
 
 
@@ -386,8 +386,8 @@ def tile_scenario_delta_gamma_losses_s7_kernel(
         for q in range(F_PASSES):
             load_shocks(q, 0)
         load_sens(0, 0)
-        load_row_constants(nc.sync, 0, 1)
         load_sens(0, 1)
+        load_row_constants(nc.sync, 0, 1)
         load_sens(1, 0)
         load_bytes(2, 1)
         load_sens(1, 1)
@@ -407,149 +407,153 @@ def tile_scenario_delta_gamma_losses_s7_kernel(
             short_cast(1, "scalar", two, two + 1)
         turn_short(0, 0)
         turn_short(1, 2)
-        shocks_interleave(0, 0, "gpsimd", 0, POOL_SHARE)
-        shocks_interleave(0, 0, "scalar", POOL_SHARE, HALF)
-        shocks_interleave(1, 0, "scalar", HEAD_SHARE, HALF)
+        for q in range(F_PASSES):
+            shocks_interleave(q, 0, "gpsimd", 0, HEAD_SHARE)
+            shocks_interleave(q, 0, "scalar", HEAD_SHARE, HALF)
         short_scale_out_both(0)
-        short_scale_out(1, 0)
+        short_scale_out_both(1)
         turn_sens(0, 0, 4)
-        shocks_interleave(1, 0, "vector", 0, HEAD_SHARE)
         shocks_quantise(0, 0)
-        shocks_quantise(1, 0)
         sens_quantise(0, 0, 0, 1)
+        shocks_quantise(1, 0)
         sens_quantise(0, 0, 1, 2)
-        row_constants(0, 1)
         turn_sens(0, 1, 6)
+        row_constants(0, 1)
         short_cast(2)
-        short_scale_out(1, 1)
-        sens_quantise(0, 1)
         short_quantise(0)
+        sens_quantise(0, 1)
 
-        spare = [(shocks_interleave, shocks_quantise, 0, 1), (shocks_interleave, shocks_quantise, 1, 1)]
-        spare = spare + [(v_interleave, v_quantise, 0, 0), (v_interleave, v_quantise, 1, 0)]
-        spare_turn = [0, 2, 3, 5]
-        for n in range(PAIRS):
-            g, pair = divmod(n, 2)
-            tiles = (2 * pair, 2 * pair + 1)
-            more_sens = g + 1 < GROUPS
-            if n == 2:
-                row_constants(1, GROUPS)
-            y_tiles(g, tiles, 0, 2 * pair)
-            if more_sens:
-                turn_sens(g + 1, pair, 4 + 2 * pair)
-            else:
-                turn_short(2 + pair, 4 + 2 * pair)
-            if n == 0:
-                short_quantise(1)
-            if n == PAIRS // 2:
-                short_order(2)
-            for (copy, quantise, x, h), turn in zip(spare, spare_turn):
-                if n == turn:
-                    copy(x, h, "vector")
-                if n == turn + 1 and n != PAIRS - 2:
-                    quantise(x, h)
-            if n in (3, 5):
-                short_cast(3, "scalar", n // 4, n // 4 + 1)
-            if n == PAIRS - 3:
-                clip_tiles(g, tiles[:1], 0)
-                sens_quantise(g + 1, pair)
-                short_order(3)
-            elif n == PAIRS - 2:
-                clip_tiles(g, tiles, 0)
-                clip_tiles(g - 1, (3,), 0)
-                v_quantise(1, 0)
-                v_interleave(2, 0, "gpsimd", 0, POOL_SHARE)
-            else:
-                clip_tiles(g, tiles, 0)
-            if more_sens:
-                if n != PAIRS - 3:
-                    sens_quantise(g + 1, pair)
-            else:
-                if pair == 1:
-                    short_quantise(2)
-                short_scale_out_both(2 + pair)
+        y_tiles(0, (0, 1), 0, 0)
+        turn_sens(1, 0, 4)
+        short_quantise(1)
+        sens_order(1, 1)
+        clip_tiles(0, (0,), 0)
+        shocks_interleave(0, 1, "vector")
+        clip_tiles(0, (1,), 0)
+        sens_quantise(1, 0)
+        y_tiles(0, (2, 3), 0, 2)
+        turn_sens(1, 1, 6)
+        row_constants(1, GROUPS)
+        turn_sens(2, 0, 4)
+        shocks_quantise(0, 1)
+        clip_tiles(0, (2, 3), 0)
+        sens_quantise(1, 1)
+        v_interleave(0, 0, "vector")
+        sens_quantise(2, 0)
+        v_quantise(0, 0)
+        y_tiles(1, (0, 1), 0, 0)
+        turn_sens(2, 1, 6)
+        y_tiles(1, (2, 3), 0, 2)
+        turn_sens(3, 0, 4)
+        shocks_interleave(1, 1, "vector")
+        clip_tiles(1, (0,), 0)
+        sens_quantise(2, 1)
+        clip_tiles(1, (1, 2, 3), 0)
+        short_order(2)
+        shocks_quantise(1, 1)
+        sens_quantise(3, 0)
+        y_tiles(2, range(PACK), 0, 0)
+        turn_sens(3, 1, 6)
+        turn_short(2, 4)
+        short_cast(3)
+        v_interleave(1, 0, "vector")
+        clip_tiles(2, (0,), 0)
+        sens_quantise(3, 1)
+        clip_tiles(2, (1, 2, 3), 0)
+        v_quantise(1, 0)
+        v_interleave(2, 0, "gpsimd", 0, POOL_SHARE)
+        short_scale_out_both(2)
+        y_tiles(3, range(PACK), 0, 0)
+        y_tiles(0, (0, 1), 1, 6)
+        y_tiles(0, (2, 3), 1, 0)
+        y_tiles(1, (0, 1), 1, 2)
+        short_order(3)
+        turn_short(3, 4)
+        clip_tiles(3, range(PACK), 0)
+        short_quantise(2)
         v_interleave(3, 0, "gpsimd", 0, POOL_SHARE)
+        short_scale_out_both(3)
         v_interleave(2, 0, "scalar", POOL_SHARE, HALF)
-        short_quantise_halves(3)
+
+        def y_group(g):
+            y_tiles(g, (0, 1), 1, 2)
+            y_tiles(g, (2, 3), 1, 6)
 
         first_tiles = range(4)
-        for g in range(GROUPS - 1):
-            if g == 1:
-                y_tiles(g, (0, 1), 1, 0)
-                short_cast(4)
-                y_tiles(g, (2, 3), 1, 2)
-            else:
-                y_tiles(g, range(PACK), 1, 0)
-            behind = (g + 2, 0) if g + 2 < GROUPS else (g - 2, 1)
-            if g == 0:
-                v_interleave(3, 0, "scalar", POOL_SHARE, HALF)
-                v_quantise(*behind)
-                clip_tiles(g, range(PACK), 1)
-            else:
-                if g == 2:
-                    v_interleave(*behind, "vector")
-                clip_tiles(g, (0, 1), 1)
-                v_quantise(*behind)
-                if g == 2:
-                    v_interleave(1, 1, "vector")
-                clip_tiles(g, (2, 3) if g == 1 else (2,), 1)
-                if g == 1:
-                    short_order(4, "scalar")
-                follow_v(first_tiles, 0, [4, 5, 6, 7], 2 * g - 2, 2 * g)
+        held = [0, 1, 4, 5]
+        v_interleave(3, 0, "scalar", POOL_SHARE, HALF)
+        short_cast(4)
+        y_tiles(1, (2, 3), 1, 6)
+        short_quantise(3, 0, 2)
+        v_quantise(2, 0)
+        short_quantise(3, 2, 4)
+        clip_tiles(0, range(PACK), 1)
+        follow_v(first_tiles, 0, held, 0, 2)
+        clip_tiles(1, (0, 1), 1)
+        v_quantise(3, 0)
+        clip_tiles(1, (2, 3), 1)
+        short_order(4, "scalar")
+        y_group(2)
+        follow_v(first_tiles, 0, held, 2, 4)
+        v_interleave(0, 1, "vector")
+        clip_tiles(2, (0, 1), 1)
+        v_quantise(0, 1)
+        v_interleave(1, 1, "vector")
+        clip_tiles(2, (2,), 1)
         short_cast(5)
         for i in first_tiles:
             loss_out(i, 0, HALF)
-        short_order(5)
         clip_tiles(2, (3,), 1)
         v_quantise(1, 1)
         v_interleave(2, 1, "gpsimd", 0, POOL_SHARE)
-        y_tiles(GROUPS - 1, range(PACK), 1, 0)
+        y_group(3)
 
-        held = [6, 7, 2, 3, 5]
-        turn_short(4, 4)
+        held = [4, 5, 6, 7, 1]
+        turn_short(4, 0)
         short_scale_out_both(4)
         short_cast(6)
         short_order(6, "scalar")
-        follow_v((0, 1), 1, held, 0, 2)
-        turn_short(5, 0)
+        follow_v((0, 1), 1, held, 0, 1)
+        turn_short(5, 2)
+        follow_v((0, 1), 1, held, 1, 2)
         short_quantise(4, 0, 2)
         v_interleave(2, 1, "vector", POOL_SHARE, HALF)
         short_quantise(4, 2, 4)
         clip_tiles(GROUPS - 1, range(PACK), 1)
         v_quantise(2, 1)
         follow_v((2, 3), 1, held, 0, 2)
-        loss_product(4, 0, HALF, 4)
+        loss_product(4, 0, HALF, 0)
         follow_v((4,), 1, held, 0, 2)
         v_interleave(3, 1, "gpsimd", 0, POOL_SHARE)
         loss_out(4, 0, HALF)
+        v_interleave(3, 1, "scalar", POOL_SHARE, HALF)
         short_scale_out_both(5)
-        short_quantise(5, 0, 2)
-        v_interleave(3, 1, "vector", POOL_SHARE, HALF)
-        short_quantise(5, 2, 4)
+        short_quantise_halves(5)
         short_cast(7)
         short_order(7, "scalar")
         follow_v(range(5), 1, held, 2, 3)
-        turn_short(6, 0)
-        loss_product(5, 0, HALF, 4)
+        short_transpose(6, 0, 0)
+        short_transpose(6, 1, 2)
+        loss_product(5, 0, HALF, 3)
         loss_out(5, 0, HALF)
         v_quantise(3, 1)
         short_scale_out_both(6)
         for i in range(5):
             follow_v((i,), 1, held, 3, 4)
             loss_out(i, HALF, HALF)
-        short_transpose(7, 0, 4)
-        short_transpose(7, 1, 6)
+        short_transpose(7, 0, 3)
+        short_transpose(7, 1, 4)
         short_quantise_halves(6)
         short_scale_out_both(7)
         short_quantise_halves(7)
-        loss_product(5, HALF, HALF, 7)
+        loss_product(5, HALF, HALF, 5)
         loss_out(5, HALF, HALF)
         for h in range(2):
-            loss_product(6, h * HALF, HALF, 2 + h)
+            loss_product(6, h * HALF, HALF, 6 + h)
             loss_out(6, h * HALF, HALF)
         quarter = HALF // 2
         for c0, width, bank, engine in (
-            (0, HALF, 5, "scalar"), (HALF, quarter, 0, "vector"), (HALF + quarter, quarter, 1, "scalar")
+            (0, HALF, 1, "scalar"), (HALF, quarter, 0, "vector"), (HALF + quarter, quarter, 2, "scalar")
         ):
             loss_product(7, c0, width, bank)
             loss_out(7, c0, width, engine)

@@ -26,14 +26,14 @@ PAIRS = 2 * GROUPS
 
 GROUPED_BUFS = 4
 TURNED_BUFS = 3
-SQUARES_BUFS = 7
+SQUARES_BUFS = 8
 V_ROWS_BUFS = 5
 WIDE_BUFS = 3
 SCALED_BUFS = 2
 ORDERED_BUFS = 3
 
 HEAD_SHARE = 224
-POOL_SHARE = 320
+POOL_SHARE = 352
 
 
 def tile_scenario_delta_gamma_losses_s7_kernel(
@@ -67,6 +67,11 @@ def tile_scenario_delta_gamma_losses_s7_kernel(
             for n in range(2):
                 sens_rows[(g, 2 * pair + n)] = rows[:, n, :]
 
+        def load_sens_tile(g, t):
+            rows = keep.tile([P, F], BF16, name="sens_tile_%d_%d" % (g, t))
+            nc.sync.dma_start(out=rows[:], in_=sens_view[g][:, t, :])
+            sens_rows[(g, t)] = rows[:]
+
         def load_shocks(q, h):
             raw = keep.tile([P, PACK, HALF], BF16, name="shocks_raw_%d_%d" % (q, h))
             nc.sync.dma_start(out=raw[:], in_=shocks_view[q][:, :, half_cols(h)])
@@ -76,14 +81,14 @@ def tile_scenario_delta_gamma_losses_s7_kernel(
             rows = keep.tile([P, n, N], U8, name="bytes_rows_%d" % i0)
             nc.sync.dma_start(out=rows[:], in_=bytes_view[:, i0 : i0 + n, :])
             for i in range(n):
-                for two in range(2):
-                    bytes_rows[(i0 + i, two)] = rows[:, i, 2 * two * K_PASS : 2 * (two + 1) * K_PASS]
-                bytes_rows[i0 + i] = rows[:, i, :]
+                for g in range(GROUPS):
+                    bytes_rows[(i0 + i, g)] = (rows[:, i, :], 0)
 
         def load_bytes_half(i, two):
             rows = keep.tile([P, 2 * K_PASS], U8, name="bytes_half_%d_%d" % (i, two))
             nc.sync.dma_start(out=rows[:], in_=bytes_view[:, i, 2 * two * K_PASS : 2 * (two + 1) * K_PASS])
-            bytes_rows[(i, two)] = rows[:]
+            for g in range(2 * two, 2 * two + 2):
+                bytes_rows[(i, g)] = (rows[:], 2 * two)
 
         def load_scale():
             nc.scalar.dma_start(
@@ -145,9 +150,10 @@ def tile_scenario_delta_gamma_losses_s7_kernel(
                 in_=shocks_grouped[(q, h)][:].rearrange("p n t -> p (n t)"),
             )
 
-        def copy_words_out(dst, bank):
+        def copy_words_out(dst, bank, engine):
             words = dst.rearrange("p q m j -> p (q m j)").bitcast(F32)
-            nc.scalar.copy(
+            copy = nc.vector.tensor_copy if engine == "vector" else nc.scalar.copy
+            copy(
                 out=words.rearrange("p (q m u) -> p q m u", q=2, u=2),
                 in_=bank.rearrange("p q u m -> p q m u"),
             )
@@ -183,12 +189,12 @@ def tile_scenario_delta_gamma_losses_s7_kernel(
                 sens_rows[(g, 2 * pair + n)] = ordered[:, n, :]
             sens_ordered.add((g, pair))
 
-        def sens_copy(g, t):
-            if t % 2 == 0:
+        def sens_copy(g, t, engine="scalar"):
+            if (g, t // 2) not in sens_grouped:
                 sens_grouped[(g, t // 2)] = work.tile(
                     [P, 2, F_PASSES, P, PACK], BF16, name="sens_grouped", align_bytes=64, bufs=TURNED_BUFS
                 )
-            copy_words_out(sens_grouped[(g, t // 2)][:, t % 2], sens_bank[(g, t)][:])
+            copy_words_out(sens_grouped[(g, t // 2)][:, t % 2], sens_bank[(g, t)][:], engine)
 
         def sens_quantise(g, pair, a0=0, a1=2):
             if (g, pair) not in sens_operand:
@@ -207,10 +213,11 @@ def tile_scenario_delta_gamma_losses_s7_kernel(
         v_rows = {}
         v_grouped = {}
 
-        def y_product(g, t, h, bank):
+        def y_product(g, t, h, bank, q0=0, q1=F_PASSES):
             codes, scales = sens_operand[(g, t // 2)]
-            y_bank[(g, t, h)] = psum.tile([P, HALF], F32, name="bank_%d" % bank)
-            for q in range(F_PASSES):
+            if q0 == 0:
+                y_bank[(g, t, h)] = psum.tile([P, HALF], F32, name="bank_%d" % bank)
+            for q in range(q0, q1):
                 nc.tensor.matmul_mx(
                     out=y_bank[(g, t, h)][:],
                     lhsT=codes[:, t % 2, q, :].bitcast(FP8X4),
@@ -255,50 +262,66 @@ def tile_scenario_delta_gamma_losses_s7_kernel(
             )
 
         short_wide = {}
-        short_ordered = set()
         short_bank = {}
+        short_ordered = set()
+        by_words = set()
         short_grouped = {}
         short_operand = {}
 
-        def short_cast(i, engine="scalar", two0=0, two1=2):
+        def short_cast(i, engine, g0=0, g1=GROUPS):
             if i not in short_wide:
-                short_wide[i] = work.tile([P, 2, 2 * K_PASS], BF16, name="short_wide", bufs=WIDE_BUFS)
-            dst = short_wide[i][:, two0:two1, :].rearrange("p a k -> p (a k)")
-            src = (bytes_rows[i] if two1 - two0 == 2 else bytes_rows[(i, two0)]).bitcast(FP8)
-            if engine == "vector":
-                nc.vector.tensor_copy(out=dst, in_=src)
-            else:
-                nc.scalar.copy(out=dst, in_=src)
+                short_wide[i] = work.tile([P, N], BF16, name="short_wide", bufs=WIDE_BUFS)
+            rows, first = bytes_rows[(i, g0)]
+            src = rows[:, (g0 - first) * K_PASS : (g1 - first) * K_PASS].bitcast(FP8)
+            copy = nc.vector.tensor_copy if engine == "vector" else nc.scalar.copy
+            copy(out=short_wide[i][:, g0 * K_PASS : g1 * K_PASS], in_=src)
 
         def short_order(i, engine="vector"):
-            wide = short_wide[i][:].rearrange("p a k -> p (a k)")
-            short_wide[i] = work.tile([P, 2, 2 * K_PASS], BF16, name="ordered", bufs=ORDERED_BUFS)
-            order_words(engine, short_wide[i][:].rearrange("p a k -> p (a k)"), wide)
+            wide = short_wide[i][:]
+            short_wide[i] = work.tile([P, N], BF16, name="ordered", bufs=ORDERED_BUFS)
+            order_words(engine, short_wide[i][:], wide)
             short_ordered.add(i)
 
-        def short_transpose(i, two, bank):
-            short_bank[(i, two)] = psum.tile([P, 2, 2, P], F32, name="bank_%d" % bank)
-            words = short_wide[i][:, two, :].bitcast(F32)
-            for q in range(2):
+        def short_turn_words(i, g0, g1, bank):
+            short_bank[(i, g0)] = psum.tile([P, 2, g1 - g0, P], F32, name="bank_%d" % bank)
+            by_words.add((i, g0))
+            words = short_wide[i][:].bitcast(F32)
+            for g in range(g0, g1):
                 for u in range(2):
                     if i in short_ordered:
-                        piece = words[:, 256 * u + P * q : 256 * u + P * (q + 1)]
+                        first = 512 * (g // 2) + 256 * u + P * (g % 2)
+                        piece = words[:, first : first + P]
                     else:
-                        piece = words[:, 256 * q + u : 256 * (q + 1) : 2]
-                    nc.tensor.transpose(short_bank[(i, two)][:, u, q, :], piece, ident[:])
+                        piece = words[:, 256 * g + u : 256 * (g + 1) : 2]
+                    nc.tensor.transpose(short_bank[(i, g0)][:, u, g - g0, :], piece, ident[:])
 
-        def short_scale_out(i, two):
-            if two == 0:
+        def short_turn(i, g0, g1, bank):
+            short_bank[(i, g0)] = psum.tile([P, g1 - g0, PACK, P], BF16, name="bank_%d" % bank)
+            for g in range(g0, g1):
+                for t in range(PACK):
+                    nc.tensor.matmul(
+                        out=short_bank[(i, g0)][:, g - g0, t, :],
+                        lhsT=short_wide[i][:, K_PASS * g + t : K_PASS * (g + 1) : PACK],
+                        rhs=ident_bf16[:],
+                        start=True,
+                        stop=True,
+                    )
+
+        def short_scale_out(i, g0, g1):
+            if g0 == 0:
                 short_grouped[i] = work.tile([P, GROUPS, P, PACK], BF16, name="short_grouped", align_bytes=64, bufs=SCALED_BUFS)
-            passes = slice(2 * two, 2 * two + 2)
-            values = short_bank[(i, two)][:].rearrange("p u q m -> p (u q m)").bitcast(BF16)
-            factors = scale_sb[:, passes, 0:PACK].rearrange("p q (u e) -> p q u e", u=2)
-            nc.vector.tensor_tensor(
-                out=short_grouped[i][:, passes].rearrange("p q m (u e) -> p q m u e", u=2),
-                in0=values.rearrange("p (u q m e) -> p q m u e", u=2, q=2, e=2),
-                in1=factors.unsqueeze(2).to_broadcast([P, 2, P, 2, 2]),
-                op=ALU.mult,
-            )
+            n = g1 - g0
+            scaled = short_grouped[i][:, g0:g1]
+            factors = scale_sb[:, g0:g1, 0:PACK]
+            if (i, g0) in by_words:
+                values = short_bank[(i, g0)][:].rearrange("p u q m -> p (u q m)").bitcast(BF16)
+                values = values.rearrange("p (u q m e) -> p q m u e", u=2, q=n, e=2)
+                scaled = scaled.rearrange("p q m (u e) -> p q m u e", u=2)
+                factors = factors.rearrange("p q (u e) -> p q u e", u=2).unsqueeze(2).to_broadcast([P, n, P, 2, 2])
+            else:
+                values = short_bank[(i, g0)][:].rearrange("p q t m -> p q m t")
+                factors = factors.unsqueeze(2).to_broadcast([P, n, P, PACK])
+            nc.vector.tensor_tensor(out=scaled, in0=values, in1=factors, op=ALU.mult)
 
         def short_quantise(i, g0=0, g1=GROUPS):
             if i not in short_operand:
@@ -315,7 +338,7 @@ def tile_scenario_delta_gamma_losses_s7_kernel(
         loss_bank = {}
         stage = []
         staged = []
-        spent = ["sens_rows_%d_%d" % (g, t0) for g in range(GROUPS) for t0 in range(2)]
+        spent = ["sens_rows_%d_%d" % (g, t0) for g in range(GROUPS) for t0 in range(2)][1:]
         spent = spent + ["shocks_raw_%d_%d" % (q, h) for h in range(2) for q in range(2)]
 
         def loss_product(i, c0, width, bank, g0=0, g1=GROUPS):
@@ -348,43 +371,15 @@ def tile_scenario_delta_gamma_losses_s7_kernel(
 
         ident = keep.tile([P, P], F32, name="ident")
         make_identity(nc, ident[:])
-
-        def turn_sens(g, pair, bank):
-            for n in range(2):
-                sens_transpose(g, 2 * pair + n, bank + n)
-                sens_copy(g, 2 * pair + n)
-
-        def turn_short(i, bank):
-            for two in range(2):
-                short_transpose(i, two, bank + two)
-
-        def short_scale_out_both(i):
-            for two in range(2):
-                short_scale_out(i, two)
-
-        def short_quantise_halves(i):
-            short_quantise(i, 0, 2)
-            short_quantise(i, 2, 4)
-
-        def y_tiles(g, tiles, h, bank):
-            for n, t in enumerate(tiles):
-                y_product(g, t, h, bank + n)
-                y_square(g, t, h)
-
-        def clip_tiles(g, tiles, h):
-            for t in tiles:
-                v_clip(g, t, h)
-
-        def follow_v(tiles, h, banks, g0, g1):
-            for i in tiles:
-                loss_product(i, h * HALF, HALF, banks[i], g0, g1)
+        ident_bf16 = keep.tile([P, P], BF16, name="ident_bf16")
+        make_identity(nc, ident_bf16[:])
 
         load_scale()
         load_bytes_half(0, 0)
         load_bytes_half(0, 1)
         load_bytes(1, 1)
-        for q in range(F_PASSES):
-            load_shocks(q, 0)
+        load_shocks(0, 0)
+        load_shocks(1, 0)
         load_sens(0, 0)
         load_sens(0, 1)
         load_row_constants(nc.sync, 0, 1)
@@ -396,164 +391,289 @@ def tile_scenario_delta_gamma_losses_s7_kernel(
         load_row_constants(nc.sync, 1, GROUPS)
         load_sens(2, 1)
         load_shocks(1, 1)
-        load_bytes(3, 1)
         load_sens(3, 0)
         load_sens(3, 1)
+        load_bytes(3, 1)
         load_bytes(4, 4)
 
-        short_cast(0, "vector", 0, 1)
+        shocks_interleave(0, 0, "gpsimd", 0, HEAD_SHARE)
+        shocks_interleave(1, 0, "gpsimd", 0, HEAD_SHARE)
         short_cast(0, "scalar", 1, 2)
-        for two in range(2):
-            short_cast(1, "scalar", two, two + 1)
-        turn_short(0, 0)
-        turn_short(1, 2)
-        for q in range(F_PASSES):
-            shocks_interleave(q, 0, "gpsimd", 0, HEAD_SHARE)
-            shocks_interleave(q, 0, "scalar", HEAD_SHARE, HALF)
-        short_scale_out_both(0)
-        short_scale_out_both(1)
-        turn_sens(0, 0, 4)
+        short_cast(0, "scalar", 2, 4)
+        short_cast(1, "scalar", 0, 2)
+        short_cast(1, "scalar", 2, 4)
+        shocks_interleave(0, 0, "scalar", HEAD_SHARE, HALF)
+        shocks_interleave(1, 0, "scalar", HEAD_SHARE, HALF)
+        short_cast(0, "vector", 0, 1)
+        short_turn_words(0, 0, 1, 6)
+        short_turn_words(0, 1, 2, 0)
+        short_turn_words(0, 2, 4, 1)
+        short_turn_words(1, 0, 2, 2)
+        short_turn_words(1, 2, 4, 3)
+        sens_transpose(0, 0, 4)
+        sens_transpose(0, 1, 5)
+        sens_copy(0, 0, "scalar")
+        sens_copy(0, 1, "scalar")
+        short_scale_out(0, 0, 1)
+        sens_transpose(0, 2, 6)
+        sens_transpose(0, 3, 7)
+        sens_copy(0, 2, "scalar")
+        sens_copy(0, 3, "scalar")
+        row_constants(0, 1)
+        short_cast(2, "scalar")
+        short_scale_out(0, 1, 2)
+        short_scale_out(0, 2, 4)
+        short_scale_out(1, 0, 2)
+        short_scale_out(1, 2, 4)
         shocks_quantise(0, 0)
+        short_quantise(0)
         sens_quantise(0, 0, 0, 1)
         shocks_quantise(1, 0)
+        y_product(0, 0, 0, 0)
+        y_square(0, 0, 0)
         sens_quantise(0, 0, 1, 2)
-        turn_sens(0, 1, 6)
-        row_constants(0, 1)
-        short_cast(2)
-        short_quantise(0)
-        sens_quantise(0, 1)
-
-        y_tiles(0, (0, 1), 0, 0)
-        turn_sens(1, 0, 4)
+        y_product(0, 1, 0, 1)
+        sens_transpose(1, 0, 4)
+        sens_transpose(1, 1, 5)
+        y_square(0, 1, 0)
+        sens_copy(1, 0, "scalar")
+        sens_copy(1, 1, "scalar")
         short_quantise(1)
-        sens_order(1, 1)
-        clip_tiles(0, (0,), 0)
+        sens_quantise(0, 1)
+        y_product(0, 2, 0, 2)
+        y_product(0, 3, 0, 3)
+        y_square(0, 2, 0)
+        y_square(0, 3, 0)
+        sens_order(1, 1, "vector")
+        sens_transpose(1, 2, 6)
+        sens_transpose(1, 3, 7)
+        sens_transpose(2, 0, 4)
+        sens_transpose(2, 1, 5)
+        sens_copy(1, 2, "scalar")
+        sens_copy(1, 3, "scalar")
+        row_constants(1, 4)
+        sens_copy(2, 0, "scalar")
+        sens_copy(2, 1, "scalar")
+        v_clip(0, 0, 0)
         shocks_interleave(0, 1, "vector")
-        clip_tiles(0, (1,), 0)
+        v_clip(0, 1, 0)
         sens_quantise(1, 0)
-        y_tiles(0, (2, 3), 0, 2)
-        turn_sens(1, 1, 6)
-        row_constants(1, GROUPS)
-        turn_sens(2, 0, 4)
+        y_product(1, 0, 0, 0)
+        y_product(1, 1, 0, 1)
+        sens_transpose(2, 2, 6)
+        sens_transpose(2, 3, 7)
+        y_square(1, 0, 0)
+        y_square(1, 1, 0)
+        sens_copy(2, 2, "scalar")
+        sens_copy(2, 3, "scalar")
         shocks_quantise(0, 1)
-        clip_tiles(0, (2, 3), 0)
+        v_clip(0, 2, 0)
+        v_clip(0, 3, 0)
         sens_quantise(1, 1)
+        y_product(1, 2, 0, 2)
+        y_product(1, 3, 0, 3)
+        sens_transpose(3, 0, 4)
+        sens_transpose(3, 1, 5)
+        y_square(1, 2, 0)
+        y_square(1, 3, 0)
+        sens_copy(3, 0, "scalar")
+        sens_copy(3, 1, "scalar")
         v_interleave(0, 0, "vector")
         sens_quantise(2, 0)
+        y_product(2, 0, 0, 0)
+        y_product(2, 1, 0, 1)
+        y_square(2, 0, 0)
+        y_square(2, 1, 0)
         v_quantise(0, 0)
-        y_tiles(1, (0, 1), 0, 0)
-        turn_sens(2, 1, 6)
-        y_tiles(1, (2, 3), 0, 2)
-        turn_sens(3, 0, 4)
         shocks_interleave(1, 1, "vector")
-        clip_tiles(1, (0,), 0)
+        v_clip(1, 0, 0)
         sens_quantise(2, 1)
-        clip_tiles(1, (1, 2, 3), 0)
-        short_order(2)
+        y_product(2, 2, 0, 2)
+        y_product(2, 3, 0, 3)
+        sens_transpose(3, 2, 6)
+        sens_transpose(3, 3, 7)
+        short_turn(2, 0, 2, 4)
+        short_turn(2, 2, 4, 5)
+        y_square(2, 2, 0)
+        y_square(2, 3, 0)
+        sens_copy(3, 2, "scalar")
+        sens_copy(3, 3, "scalar")
+        short_cast(3, "scalar")
+        v_clip(1, 1, 0)
+        v_clip(1, 2, 0)
+        v_clip(1, 3, 0)
         shocks_quantise(1, 1)
         sens_quantise(3, 0)
-        y_tiles(2, range(PACK), 0, 0)
-        turn_sens(3, 1, 6)
-        turn_short(2, 4)
-        short_cast(3)
+        y_product(3, 0, 0, 0)
+        y_product(3, 1, 0, 1)
+        y_square(3, 0, 0)
+        y_square(3, 1, 0)
         v_interleave(1, 0, "vector")
-        clip_tiles(2, (0,), 0)
+        v_clip(2, 0, 0)
         sens_quantise(3, 1)
-        clip_tiles(2, (1, 2, 3), 0)
-        v_quantise(1, 0)
+        y_product(3, 2, 0, 2)
+        y_product(3, 3, 0, 3)
+        y_product(0, 0, 1, 6)
+        y_product(0, 1, 1, 7)
+        y_product(0, 2, 1, 0)
+        y_product(0, 3, 1, 1)
+        y_square(3, 2, 0)
+        y_product(1, 0, 1, 2)
+        y_square(3, 3, 0)
+        y_product(1, 1, 1, 3)
+        y_square(0, 0, 1)
+        v_clip(2, 1, 0)
+        y_square(0, 1, 1)
+        v_clip(2, 2, 0)
+        y_square(0, 2, 1)
+        v_clip(2, 3, 0)
         v_interleave(2, 0, "gpsimd", 0, POOL_SHARE)
-        short_scale_out_both(2)
-        y_tiles(3, range(PACK), 0, 0)
-        y_tiles(0, (0, 1), 1, 6)
-        y_tiles(0, (2, 3), 1, 0)
-        y_tiles(1, (0, 1), 1, 2)
-        short_order(3)
-        turn_short(3, 4)
-        clip_tiles(3, range(PACK), 0)
-        short_quantise(2)
-        v_interleave(3, 0, "gpsimd", 0, POOL_SHARE)
-        short_scale_out_both(3)
+        y_square(0, 3, 1)
+        v_quantise(1, 0)
+        short_scale_out(2, 0, 2)
+        short_turn(3, 0, 2, 4)
+        short_scale_out(2, 2, 4)
+        short_turn(3, 2, 4, 5)
+        y_product(1, 2, 1, 6)
+        y_product(1, 3, 1, 7)
+        loss_product(0, 0, HALF, 0, 0, 2)
+        loss_product(1, 0, HALF, 1, 0, 2)
+        v_clip(3, 0, 0)
+        y_square(1, 0, 1)
+        v_clip(3, 1, 0)
+        y_square(1, 1, 1)
         v_interleave(2, 0, "scalar", POOL_SHARE, HALF)
-
-        def y_group(g):
-            y_tiles(g, (0, 1), 1, 2)
-            y_tiles(g, (2, 3), 1, 6)
-
-        first_tiles = range(4)
-        held = [0, 1, 4, 5]
+        v_clip(3, 2, 0)
+        v_clip(3, 3, 0)
+        v_interleave(3, 0, "gpsimd", 0, POOL_SHARE)
         v_interleave(3, 0, "scalar", POOL_SHARE, HALF)
-        short_cast(4)
-        y_tiles(1, (2, 3), 1, 6)
+        short_cast(4, "scalar")
+        y_square(1, 2, 1)
+        y_square(1, 3, 1)
+        short_order(4, "scalar")
+        short_quantise(2)
+        short_scale_out(3, 0, 2)
+        loss_product(2, 0, HALF, 4, 0, 2)
+        short_scale_out(3, 2, 4)
         short_quantise(3, 0, 2)
+        loss_product(3, 0, HALF, 5, 0, 2)
+        y_product(2, 0, 1, 2)
+        y_product(2, 1, 1, 3)
+        y_product(2, 2, 1, 6)
+        y_product(2, 3, 1, 7)
         v_quantise(2, 0)
         short_quantise(3, 2, 4)
-        clip_tiles(0, range(PACK), 1)
-        follow_v(first_tiles, 0, held, 0, 2)
-        clip_tiles(1, (0, 1), 1)
+        v_clip(0, 0, 1)
+        y_square(2, 0, 1)
+        v_clip(0, 1, 1)
+        y_square(2, 1, 1)
+        v_clip(0, 2, 1)
+        y_square(2, 2, 1)
+        v_clip(0, 3, 1)
+        y_square(2, 3, 1)
+        short_cast(5, "scalar")
+        v_clip(1, 0, 1)
+        v_clip(1, 1, 1)
         v_quantise(3, 0)
-        clip_tiles(1, (2, 3), 1)
-        short_order(4, "scalar")
-        y_group(2)
-        follow_v(first_tiles, 0, held, 2, 4)
-        v_interleave(0, 1, "vector")
-        clip_tiles(2, (0, 1), 1)
-        v_quantise(0, 1)
-        v_interleave(1, 1, "vector")
-        clip_tiles(2, (2,), 1)
-        short_cast(5)
-        for i in first_tiles:
-            loss_out(i, 0, HALF)
-        clip_tiles(2, (3,), 1)
-        v_quantise(1, 1)
-        v_interleave(2, 1, "gpsimd", 0, POOL_SHARE)
-        y_group(3)
-
-        held = [4, 5, 6, 7, 1]
-        turn_short(4, 0)
-        short_scale_out_both(4)
-        short_cast(6)
+        loss_product(0, 0, HALF, 0, 2, 4)
+        loss_product(1, 0, HALF, 1, 2, 4)
+        loss_product(2, 0, HALF, 4, 2, 4)
+        loss_product(3, 0, HALF, 5, 2, 4)
+        y_product(3, 0, 1, 2)
+        y_product(3, 1, 1, 3)
+        y_product(3, 2, 1, 6)
+        y_product(3, 3, 1, 7)
+        loss_out(0, 0, HALF, "scalar")
+        short_turn_words(4, 0, 2, 0)
+        loss_out(1, 0, HALF, "scalar")
+        short_turn_words(4, 2, 4, 1)
+        loss_out(2, 0, HALF, "scalar")
+        loss_out(3, 0, HALF, "scalar")
+        y_square(3, 0, 1)
+        y_square(3, 1, 1)
+        v_clip(1, 2, 1)
+        y_square(3, 2, 1)
+        v_clip(1, 3, 1)
+        y_square(3, 3, 1)
+        short_cast(6, "scalar")
         short_order(6, "scalar")
-        follow_v((0, 1), 1, held, 0, 1)
-        turn_short(5, 2)
-        follow_v((0, 1), 1, held, 1, 2)
+        v_interleave(0, 1, "vector")
+        v_clip(2, 0, 1)
+        v_clip(2, 1, 1)
+        v_quantise(0, 1)
+        loss_product(0, 512, HALF, 4, 0, 1)
+        loss_product(1, 512, HALF, 5, 0, 1)
+        short_turn_words(5, 0, 2, 2)
+        short_turn_words(5, 2, 4, 3)
+        v_interleave(1, 1, "vector")
+        v_clip(2, 2, 1)
+        v_clip(2, 3, 1)
+        v_interleave(2, 1, "gpsimd", 0, POOL_SHARE)
+        v_quantise(1, 1)
+        loss_product(0, 512, HALF, 4, 1, 2)
+        loss_product(1, 512, HALF, 5, 1, 2)
+        loss_product(2, 512, HALF, 6, 0, 2)
+        loss_product(3, 512, HALF, 7, 0, 2)
+        short_scale_out(4, 0, 2)
+        short_scale_out(4, 2, 4)
         short_quantise(4, 0, 2)
         v_interleave(2, 1, "vector", POOL_SHARE, HALF)
         short_quantise(4, 2, 4)
-        clip_tiles(GROUPS - 1, range(PACK), 1)
-        v_quantise(2, 1)
-        follow_v((2, 3), 1, held, 0, 2)
-        loss_product(4, 0, HALF, 0)
-        follow_v((4,), 1, held, 0, 2)
+        loss_product(4, 0, HALF, 0, 0, 4)
+        loss_product(4, 512, HALF, 1, 0, 2)
+        loss_out(4, 0, HALF, "scalar")
+        v_clip(3, 0, 1)
+        v_clip(3, 1, 1)
+        v_clip(3, 2, 1)
+        v_clip(3, 3, 1)
         v_interleave(3, 1, "gpsimd", 0, POOL_SHARE)
-        loss_out(4, 0, HALF)
         v_interleave(3, 1, "scalar", POOL_SHARE, HALF)
-        short_scale_out_both(5)
-        short_quantise_halves(5)
-        short_cast(7)
+        short_cast(7, "scalar")
         short_order(7, "scalar")
-        follow_v(range(5), 1, held, 2, 3)
-        short_transpose(6, 0, 0)
-        short_transpose(6, 1, 2)
-        loss_product(5, 0, HALF, 3)
-        loss_out(5, 0, HALF)
+        v_quantise(2, 1)
+        loss_product(0, 512, HALF, 4, 2, 3)
+        loss_product(1, 512, HALF, 5, 2, 3)
+        loss_product(2, 512, HALF, 6, 2, 3)
+        loss_product(3, 512, HALF, 7, 2, 3)
+        loss_product(4, 512, HALF, 1, 2, 3)
+        short_turn_words(6, 0, 2, 0)
+        short_scale_out(5, 0, 2)
+        short_turn_words(6, 2, 4, 2)
+        short_scale_out(5, 2, 4)
+        short_quantise(5, 0, 2)
+        short_quantise(5, 2, 4)
+        loss_product(5, 0, HALF, 3, 0, 4)
+        loss_out(5, 0, HALF, "scalar")
         v_quantise(3, 1)
-        short_scale_out_both(6)
-        for i in range(5):
-            follow_v((i,), 1, held, 3, 4)
-            loss_out(i, HALF, HALF)
-        short_transpose(7, 0, 3)
-        short_transpose(7, 1, 4)
-        short_quantise_halves(6)
-        short_scale_out_both(7)
-        short_quantise_halves(7)
-        loss_product(5, HALF, HALF, 5)
-        loss_out(5, HALF, HALF)
-        for h in range(2):
-            loss_product(6, h * HALF, HALF, 6 + h)
-            loss_out(6, h * HALF, HALF)
-        quarter = HALF // 2
-        for c0, width, bank, engine in (
-            (0, HALF, 1, "scalar"), (HALF, quarter, 0, "vector"), (HALF + quarter, quarter, 2, "scalar")
-        ):
-            loss_product(7, c0, width, bank)
-            loss_out(7, c0, width, engine)
+        loss_product(0, 512, HALF, 4, 3, 4)
+        loss_product(1, 512, HALF, 5, 3, 4)
+        loss_product(2, 512, HALF, 6, 3, 4)
+        loss_product(3, 512, HALF, 7, 3, 4)
+        loss_product(4, 512, HALF, 1, 3, 4)
+        short_turn_words(7, 0, 2, 3)
+        loss_out(0, 512, HALF, "scalar")
+        short_turn_words(7, 2, 4, 4)
+        loss_out(1, 512, HALF, "scalar")
+        loss_product(5, 512, HALF, 5, 0, 4)
+        loss_out(2, 512, HALF, "scalar")
+        loss_out(3, 512, HALF, "scalar")
+        loss_out(4, 512, HALF, "scalar")
+        loss_out(5, 512, HALF, "scalar")
+        short_scale_out(6, 0, 2)
+        short_scale_out(6, 2, 4)
+        short_quantise(6, 0, 2)
+        short_quantise(6, 2, 4)
+        loss_product(6, 0, HALF, 6, 0, 4)
+        loss_product(6, 512, HALF, 7, 0, 4)
+        loss_out(6, 0, HALF, "scalar")
+        loss_out(6, 512, HALF, "scalar")
+        short_scale_out(7, 0, 2)
+        short_scale_out(7, 2, 4)
+        short_quantise(7, 0, 2)
+        short_quantise(7, 2, 4)
+        loss_product(7, 0, HALF, 1, 0, 4)
+        loss_product(7, 512, 256, 0)
+        loss_product(7, 768, 256, 2)
+        loss_out(7, 0, HALF, "scalar")
+        loss_out(7, 512, 256, "vector")
+        loss_out(7, 768, 256, "scalar")

@@ -33,7 +33,7 @@ SCALED_BUFS = 2
 ORDERED_BUFS = 3
 
 HEAD_SHARE = 224
-POOL_SHARE = 352
+POOL_SHARE = 384
 
 
 def tile_scenario_delta_gamma_losses_s7_kernel(
@@ -433,17 +433,18 @@ def tile_scenario_delta_gamma_losses_s7_kernel(
         y_square(0, 0, 0)
         sens_quantise(0, 0, 1, 2)
         y_product(0, 1, 0, 1)
+        y_square(0, 1, 0)
+        sens_order(1, 0, "vector")
         sens_transpose(1, 0, 4)
         sens_transpose(1, 1, 5)
-        y_square(0, 1, 0)
         sens_copy(1, 0, "scalar")
         sens_copy(1, 1, "scalar")
-        short_quantise(1)
         sens_quantise(0, 1)
         y_product(0, 2, 0, 2)
         y_product(0, 3, 0, 3)
         y_square(0, 2, 0)
         y_square(0, 3, 0)
+        short_quantise(1)
         sens_order(1, 1, "vector")
         sens_transpose(1, 2, 6)
         sens_transpose(1, 3, 7)
@@ -485,7 +486,6 @@ def tile_scenario_delta_gamma_losses_s7_kernel(
         y_square(2, 0, 0)
         y_square(2, 1, 0)
         v_quantise(0, 0)
-        shocks_interleave(1, 1, "vector")
         v_clip(1, 0, 0)
         sens_quantise(2, 1)
         y_product(2, 2, 0, 2)
@@ -499,6 +499,7 @@ def tile_scenario_delta_gamma_losses_s7_kernel(
         sens_copy(3, 2, "scalar")
         sens_copy(3, 3, "scalar")
         short_cast(3, "scalar")
+        shocks_interleave(1, 1, "vector")
         v_clip(1, 1, 0)
         v_clip(1, 2, 0)
         v_clip(1, 3, 0)

from contextlib import ExitStack

import concourse.mybir as mybir
from concourse.masks import make_identity

N, F, S, B = 2048, 1024, 1024, 1024
FLOPS = 2 * N * F * S + 2 * B * N * S

F32 = mybir.dt.float32
BF16 = mybir.dt.bfloat16
U32 = mybir.dt.uint32
U8 = mybir.dt.uint8
FP8 = mybir.dt.float8_e4m3fn
FP8X4 = mybir.dt.float8_e4m3fn_x4
ALU = mybir.AluOpType
ACT = mybir.ActivationFunctionType

P = 128
PACK = 4
K_PASS = P * PACK
F_PASSES = F // K_PASS
GROUPS = N // K_PASS
HALF = S // 2
BOOK_TILES = B // P
PAIRS = 2 * GROUPS

GROUPED_BUFS = 4
TURNED_BUFS = 3
SQUARES_BUFS = 8
V_ROWS_BUFS = 5
WIDE_BUFS = 3
SCALED_BUFS = 2
ORDERED_BUFS = 3

HEAD_SHARE = 224
POOL_SHARE = 384


def tile_scenario_delta_gamma_losses_s7_kernel(
    tc, sens, shocks, tilt, cap, short_bytes, short_scale, out
):
    nc = tc.nc
    with ExitStack() as ctx:
        keep = ctx.enter_context(tc.tile_pool(name="keep", bufs=1))
        work = ctx.enter_context(tc.tile_pool(name="work", bufs=2))
        psum = ctx.enter_context(tc.psum_pool(name="psum", bufs=1))
        ctx.enter_context(tc.manual_schedule())

        sens_view = sens.rearrange("(g m t) k -> g m t k", m=P, t=PACK)
        shocks_view = shocks.rearrange("(g p t) s -> g p t s", p=P, t=PACK)
        bytes_view = short_bytes.rearrange("(i p) k -> p i k", p=P)
        sens_rows = {}
        sens_pairs = {}
        shocks_raw = {}
        bytes_rows = {}
        scale_sb = keep.tile([P, GROUPS, 8], F32, name="scale_sb")
        tilt_raw = keep.tile([P, GROUPS, 16], BF16, name="tilt_raw")
        cap_raw = keep.tile([P, GROUPS, 16], BF16, name="cap_raw")

        def half_cols(h):
            return slice(h * HALF, (h + 1) * HALF)

        def load_sens(g, pair):
            rows = keep.tile([P, 2, F], BF16, name="sens_rows_%d_%d" % (g, pair))
            nc.sync.dma_start(out=rows[:], in_=sens_view[g][:, 2 * pair : 2 * pair + 2, :])
            sens_pairs[(g, pair)] = rows[:].rearrange("p a k -> p (a k)")
            for n in range(2):
                sens_rows[(g, 2 * pair + n)] = rows[:, n, :]

        def load_sens_tile(g, t):
            rows = keep.tile([P, F], BF16, name="sens_tile_%d_%d" % (g, t))
            nc.sync.dma_start(out=rows[:], in_=sens_view[g][:, t, :])
            sens_rows[(g, t)] = rows[:]

        def load_shocks(q, h):
            raw = keep.tile([P, PACK, HALF], BF16, name="shocks_raw_%d_%d" % (q, h))
            nc.sync.dma_start(out=raw[:], in_=shocks_view[q][:, :, half_cols(h)])
            shocks_raw[(q, h)] = raw

        def load_bytes(i0, n):
            rows = keep.tile([P, n, N], U8, name="bytes_rows_%d" % i0)
            nc.sync.dma_start(out=rows[:], in_=bytes_view[:, i0 : i0 + n, :])
            for i in range(n):
                for g in range(GROUPS):
                    bytes_rows[(i0 + i, g)] = (rows[:, i, :], 0)

        def load_bytes_half(i, two):
            rows = keep.tile([P, 2 * K_PASS], U8, name="bytes_half_%d_%d" % (i, two))
            nc.sync.dma_start(out=rows[:], in_=bytes_view[:, i, 2 * two * K_PASS : 2 * (two + 1) * K_PASS])
            for g in range(2 * two, 2 * two + 2):
                bytes_rows[(i, g)] = (rows[:], 2 * two)

        def load_scale():
            nc.scalar.dma_start(
                out=scale_sb[:, :, 0:PACK], in_=short_scale.rearrange("o (g p t) -> p (o g) t", p=P, t=PACK)
            )

        def load_row_constants(queue, g0, g1):
            for raw, vector in ((tilt_raw, tilt), (cap_raw, cap)):
                queue.dma_start(
                    out=raw[:, g0:g1, 0:PACK], in_=vector.rearrange("(g m t) -> m g t", m=P, t=PACK)[:, g0:g1, :]
                )

        half_tilt = keep.tile([P, GROUPS, PACK], F32, name="half_tilt")
        half_tilt_sq = keep.tile([P, GROUPS, PACK], F32, name="half_tilt_sq")
        cap_f32 = keep.tile([P, GROUPS, PACK], F32, name="cap_f32")

        def row_constants(g0, g1):
            raw = tilt_raw[:, g0:g1, 0:PACK]
            nc.scalar.activation(out=half_tilt[:, g0:g1], in_=raw, func=ACT.Copy, scale=0.5)
            nc.scalar.activation(out=half_tilt_sq[:, g0:g1], in_=raw, func=ACT.Square, scale=0.5)
            nc.scalar.copy(out=cap_f32[:, g0:g1], in_=cap_raw[:, g0:g1, 0:PACK])

        shocks_codes = keep.tile([P, F_PASSES, S], U32, name="shocks_codes", align_bytes=64)
        shocks_scales = keep.tile([P, F_PASSES, S], U8, name="shocks_scales", align_bytes=64)
        v_codes = [keep.tile([P, S], U32, name="v_codes_%d" % g, align_bytes=64) for g in range(GROUPS)]
        v_scales = [keep.tile([P, S], U8, name="v_scales_%d" % g, align_bytes=64) for g in range(GROUPS)]

        def interleave(engine, dst, src, c0, c1):
            d = dst.rearrange("p (b c) t -> p b t c", c=4)[:, c0 // 4 : c1 // 4]
            s = src.rearrange("p t (b c) -> p b t c", c=4)[:, c0 // 4 : c1 // 4]
            if engine == "vector":
                nc.vector.tensor_copy(out=d, in_=s)
            elif engine == "scalar":
                nc.scalar.copy(out=d, in_=s)
            else:
                nc.gpsimd.tensor_scalar(
                    out=dst[:, c0:c1, :],
                    in0=src[:, :, c0:c1].rearrange("p t n -> p n t"),
                    scalar1=1.0,
                    scalar2=0.0,
                    op0=ALU.mult,
                    op1=ALU.add,
                )

        def grouped_tile():
            return work.tile([P, HALF, PACK], BF16, name="grouped", align_bytes=64, bufs=GROUPED_BUFS)

        shocks_grouped = {}

        def shocks_interleave(q, h, engine, c0=0, c1=HALF):
            if (q, h) not in shocks_grouped:
                shocks_grouped[(q, h)] = grouped_tile()
            interleave(engine, shocks_grouped[(q, h)][:], shocks_raw[(q, h)][:], c0, c1)

        def shocks_quantise(q, h):
            nc.vector.quantize_mx(
                out=shocks_codes[:, q, half_cols(h)].bitcast(FP8X4),
                scales=shocks_scales[:, q, half_cols(h)],
                in_=shocks_grouped[(q, h)][:].rearrange("p n t -> p (n t)"),
            )

        def copy_words_out(dst, bank, engine):
            words = dst.rearrange("p q m j -> p (q m j)").bitcast(F32)
            copy = nc.vector.tensor_copy if engine == "vector" else nc.scalar.copy
            copy(
                out=words.rearrange("p (q m u) -> p q m u", q=2, u=2),
                in_=bank.rearrange("p q u m -> p q m u"),
            )

        sens_bank = {}
        sens_grouped = {}
        sens_operand = {}
        sens_ordered = set()

        def sens_transpose(g, t, bank):
            sens_bank[(g, t)] = psum.tile([P, F_PASSES, 2, P], F32, name="bank_%d" % bank)
            words = sens_rows[(g, t)].bitcast(F32)
            for q in range(F_PASSES):
                for u in range(2):
                    if (g, t // 2) in sens_ordered:
                        piece = words[:, 256 * u + P * q : 256 * u + P * (q + 1)]
                    else:
                        piece = words[:, 256 * q + u : 256 * (q + 1) : 2]
                    nc.tensor.transpose(sens_bank[(g, t)][:, q, u, :], piece, ident[:])

        def order_words(engine, dst, src):
            d = dst.bitcast(F32).rearrange("p (a u m) -> p a u m", a=2, u=2)
            s = src.bitcast(F32).rearrange("p (a m u) -> p a u m", a=2, u=2)
            if engine == "vector":
                nc.vector.tensor_copy(out=d, in_=s)
            else:
                nc.scalar.copy(out=d, in_=s)

        def sens_order(g, pair, engine="vector"):
            ordered = work.tile([P, 2, F], BF16, name="ordered", bufs=ORDERED_BUFS)
            order_words(engine, ordered[:].rearrange("p a k -> p (a k)"), sens_pairs[(g, pair)])
            for n in range(2):
                sens_rows[(g, 2 * pair + n)] = ordered[:, n, :]
            sens_ordered.add((g, pair))

        def sens_copy(g, t, engine="scalar"):
            if (g, t // 2) not in sens_grouped:
                sens_grouped[(g, t // 2)] = work.tile(
                    [P, 2, F_PASSES, P, PACK], BF16, name="sens_grouped", align_bytes=64, bufs=TURNED_BUFS
                )
            copy_words_out(sens_grouped[(g, t // 2)][:, t % 2], sens_bank[(g, t)][:], engine)

        def sens_quantise(g, pair, a0=0, a1=2):
            if (g, pair) not in sens_operand:
                codes = keep.tile([P, 2, F_PASSES, P], U32, name="sens_codes_%d_%d" % (g, pair), align_bytes=64)
                scales = keep.tile([P, 2, F_PASSES, P], U8, name="sens_scales_%d_%d" % (g, pair), align_bytes=64)
                sens_operand[(g, pair)] = (codes, scales)
            codes, scales = sens_operand[(g, pair)]
            nc.vector.quantize_mx(
                out=codes[:, a0:a1].rearrange("p a q m -> p (a q m)").bitcast(FP8X4),
                scales=scales[:, a0:a1].rearrange("p a q m -> p (a q m)"),
                in_=sens_grouped[(g, pair)][:, a0:a1].rearrange("p a q m j -> p (a q m j)"),
            )

        y_bank = {}
        squares = {}
        v_rows = {}
        v_grouped = {}

        def y_product(g, t, h, bank, q0=0, q1=F_PASSES):
            codes, scales = sens_operand[(g, t // 2)]
            if q0 == 0:
                y_bank[(g, t, h)] = psum.tile([P, HALF], F32, name="bank_%d" % bank)
            for q in range(q0, q1):
                nc.tensor.matmul_mx(
                    out=y_bank[(g, t, h)][:],
                    lhsT=codes[:, t % 2, q, :].bitcast(FP8X4),
                    lhsT_scale=scales[:, t % 2, q, :],
                    rhs=shocks_codes[:, q, half_cols(h)].bitcast(FP8X4),
                    rhs_scale=shocks_scales[:, q, half_cols(h)],
                    start=(q == 0),
                    stop=(q == F_PASSES - 1),
                )

        def y_square(g, t, h):
            squares[(g, t, h)] = work.tile([P, HALF], F32, name="squares", bufs=SQUARES_BUFS)
            nc.scalar.activation(
                out=squares[(g, t, h)][:],
                in_=y_bank[(g, t, h)][:],
                func=ACT.Square,
                bias=half_tilt[:, g, t : t + 1],
            )

        def v_clip(g, t, h):
            if (g, h) not in v_rows:
                v_rows[(g, h)] = work.tile([P, PACK, HALF], BF16, name="v_rows", bufs=V_ROWS_BUFS)
            nc.vector.tensor_scalar(
                out=v_rows[(g, h)][:, t, :],
                in0=squares[(g, t, h)][:],
                scalar1=half_tilt_sq[:, g, t : t + 1],
                scalar2=cap_f32[:, g, t : t + 1],
                op0=ALU.subtract,
                op1=ALU.min,
            )

        def v_interleave(g, h, engine, c0=0, c1=HALF):
            if (g, h) not in v_grouped:
                v_grouped[(g, h)] = grouped_tile()
            interleave(engine, v_grouped[(g, h)][:], v_rows[(g, h)][:], c0, c1)

        def v_quantise(g, h):
            nc.vector.quantize_mx(
                out=v_codes[g][:, half_cols(h)].bitcast(FP8X4),
                scales=v_scales[g][:, half_cols(h)],
                in_=v_grouped[(g, h)][:].rearrange("p n t -> p (n t)"),
            )

        short_wide = {}
        short_bank = {}
        short_ordered = set()
        by_words = set()
        short_grouped = {}
        short_operand = {}

        def short_cast(i, engine, g0=0, g1=GROUPS):
            if i not in short_wide:
                short_wide[i] = work.tile([P, N], BF16, name="short_wide", bufs=WIDE_BUFS)
            rows, first = bytes_rows[(i, g0)]
            src = rows[:, (g0 - first) * K_PASS : (g1 - first) * K_PASS].bitcast(FP8)
            copy = nc.vector.tensor_copy if engine == "vector" else nc.scalar.copy
            copy(out=short_wide[i][:, g0 * K_PASS : g1 * K_PASS], in_=src)

        def short_order(i, engine="vector"):
            wide = short_wide[i][:]
            short_wide[i] = work.tile([P, N], BF16, name="ordered", bufs=ORDERED_BUFS)
            order_words(engine, short_wide[i][:], wide)
            short_ordered.add(i)

        def short_turn_words(i, g0, g1, bank):
            short_bank[(i, g0)] = psum.tile([P, 2, g1 - g0, P], F32, name="bank_%d" % bank)
            by_words.add((i, g0))
            words = short_wide[i][:].bitcast(F32)
            for g in range(g0, g1):
                for u in range(2):
                    if i in short_ordered:
                        first = 512 * (g // 2) + 256 * u + P * (g % 2)
                        piece = words[:, first : first + P]
                    else:
                        piece = words[:, 256 * g + u : 256 * (g + 1) : 2]
                    nc.tensor.transpose(short_bank[(i, g0)][:, u, g - g0, :], piece, ident[:])

        def short_turn(i, g0, g1, bank):
            short_bank[(i, g0)] = psum.tile([P, g1 - g0, PACK, P], BF16, name="bank_%d" % bank)
            for g in range(g0, g1):
                for t in range(PACK):
                    nc.tensor.matmul(
                        out=short_bank[(i, g0)][:, g - g0, t, :],
                        lhsT=short_wide[i][:, K_PASS * g + t : K_PASS * (g + 1) : PACK],
                        rhs=ident_bf16[:],
                        start=True,
                        stop=True,
                    )

        def short_scale_out(i, g0, g1):
            if g0 == 0:
                short_grouped[i] = work.tile([P, GROUPS, P, PACK], BF16, name="short_grouped", align_bytes=64, bufs=SCALED_BUFS)
            n = g1 - g0
            scaled = short_grouped[i][:, g0:g1]
            factors = scale_sb[:, g0:g1, 0:PACK]
            if (i, g0) in by_words:
                values = short_bank[(i, g0)][:].rearrange("p u q m -> p (u q m)").bitcast(BF16)
                values = values.rearrange("p (u q m e) -> p q m u e", u=2, q=n, e=2)
                scaled = scaled.rearrange("p q m (u e) -> p q m u e", u=2)
                factors = factors.rearrange("p q (u e) -> p q u e", u=2).unsqueeze(2).to_broadcast([P, n, P, 2, 2])
            else:
                values = short_bank[(i, g0)][:].rearrange("p q t m -> p q m t")
                factors = factors.unsqueeze(2).to_broadcast([P, n, P, PACK])
            nc.vector.tensor_tensor(out=scaled, in0=values, in1=factors, op=ALU.mult)

        def short_quantise(i, g0=0, g1=GROUPS):
            if i not in short_operand:
                codes = work.tile([P, GROUPS, P], U32, name="short_codes", align_bytes=64, bufs=BOOK_TILES)
                scales = work.tile([P, GROUPS, P], U8, name="short_scales", align_bytes=64, bufs=BOOK_TILES)
                short_operand[i] = (codes, scales)
            codes, scales = short_operand[i]
            nc.vector.quantize_mx(
                out=codes[:, g0:g1].rearrange("p g m -> p (g m)").bitcast(FP8X4),
                scales=scales[:, g0:g1].rearrange("p g m -> p (g m)"),
                in_=short_grouped[i][:, g0:g1].rearrange("p g m j -> p (g m j)"),
            )

        loss_bank = {}
        stage = []
        staged = []
        spent = ["sens_rows_%d_%d" % (g, t0) for g in range(GROUPS) for t0 in range(2)][1:]
        spent = spent + ["shocks_raw_%d_%d" % (q, h) for h in range(2) for q in range(2)]

        def loss_product(i, c0, width, bank, g0=0, g1=GROUPS):
            codes, scales = short_operand[i]
            cols = slice(c0, c0 + width)
            if g0 == 0:
                loss_bank[(i, c0)] = psum.tile([P, width], F32, name="bank_%d" % bank)
            for g in range(g0, g1):
                nc.tensor.matmul_mx(
                    out=loss_bank[(i, c0)][:],
                    lhsT=codes[:, g, :].bitcast(FP8X4),
                    lhsT_scale=scales[:, g, :],
                    rhs=v_codes[g][:, cols].bitcast(FP8X4),
                    rhs_scale=v_scales[g][:, cols],
                    start=(g == 0),
                    stop=(g == GROUPS - 1),
                )

        def loss_out(i, c0, width, engine="scalar", queue=nc.sync):
            n = len(staged)
            if n % 2 == 0:
                stage.append(keep.tile([P, 2, HALF], F32, name=spent[n // 2]))
            rows = stage[-1][:, n % 2, 0:width]
            staged.append((i, c0))
            if engine == "vector":
                nc.vector.tensor_copy(out=rows, in_=loss_bank[(i, c0)][:])
            else:
                nc.scalar.copy(out=rows, in_=loss_bank[(i, c0)][:])
            queue.dma_start(out=out[i * P : (i + 1) * P, c0 : c0 + width], in_=rows)

        ident = keep.tile([P, P], F32, name="ident")
        make_identity(nc, ident[:])
        ident_bf16 = keep.tile([P, P], BF16, name="ident_bf16")
        make_identity(nc, ident_bf16[:])

        load_scale()
        load_bytes_half(0, 0)
        load_bytes_half(0, 1)
        load_bytes(1, 1)
        load_shocks(0, 0)
        load_shocks(1, 0)
        load_sens(0, 0)
        load_sens(0, 1)
        load_row_constants(nc.sync, 0, 1)
        load_sens(1, 0)
        load_bytes(2, 1)
        load_sens(1, 1)
        load_shocks(0, 1)
        load_sens(2, 0)
        load_row_constants(nc.sync, 1, GROUPS)
        load_sens(2, 1)
        load_shocks(1, 1)
        load_sens(3, 0)
        load_sens(3, 1)
        load_bytes(3, 1)
        load_bytes(4, 4)

        shocks_interleave(0, 0, "gpsimd", 0, HEAD_SHARE)
        shocks_interleave(1, 0, "gpsimd", 0, HEAD_SHARE)
        short_cast(0, "scalar", 1, 2)
        short_cast(0, "scalar", 2, 4)
        short_cast(1, "scalar", 0, 2)
        short_cast(1, "scalar", 2, 4)
        shocks_interleave(0, 0, "scalar", HEAD_SHARE, HALF)
        shocks_interleave(1, 0, "scalar", HEAD_SHARE, HALF)
        short_cast(0, "vector", 0, 1)
        short_turn_words(0, 0, 1, 6)
        short_turn_words(0, 1, 2, 0)
        short_turn_words(0, 2, 4, 1)
        short_turn_words(1, 0, 2, 2)
        short_turn_words(1, 2, 4, 3)
        sens_transpose(0, 0, 4)
        sens_transpose(0, 1, 5)
        sens_copy(0, 0, "scalar")
        sens_copy(0, 1, "scalar")
        short_scale_out(0, 0, 1)
        sens_transpose(0, 2, 6)
        sens_transpose(0, 3, 7)
        sens_copy(0, 2, "scalar")
        sens_copy(0, 3, "scalar")
        row_constants(0, 1)
        short_cast(2, "scalar")
        short_scale_out(0, 1, 2)
        short_scale_out(0, 2, 4)
        short_scale_out(1, 0, 2)
        short_scale_out(1, 2, 4)
        shocks_quantise(0, 0)
        short_quantise(0)
        sens_quantise(0, 0, 0, 1)
        shocks_quantise(1, 0)
        y_product(0, 0, 0, 0)
        y_square(0, 0, 0)
        sens_quantise(0, 0, 1, 2)
        y_product(0, 1, 0, 1)
        y_square(0, 1, 0)
        sens_order(1, 0, "vector")
        sens_transpose(1, 0, 4)
        sens_transpose(1, 1, 5)
        sens_copy(1, 0, "scalar")
        sens_copy(1, 1, "scalar")
        sens_quantise(0, 1)
        y_product(0, 2, 0, 2)
        y_product(0, 3, 0, 3)
        y_square(0, 2, 0)
        y_square(0, 3, 0)
        short_quantise(1)
        sens_order(1, 1, "vector")
        sens_transpose(1, 2, 6)
        sens_transpose(1, 3, 7)
        sens_transpose(2, 0, 4)
        sens_transpose(2, 1, 5)
        sens_copy(1, 2, "scalar")
        sens_copy(1, 3, "scalar")
        row_constants(1, 4)
        sens_copy(2, 0, "scalar")
        sens_copy(2, 1, "scalar")
        v_clip(0, 0, 0)
        shocks_interleave(0, 1, "vector")
        v_clip(0, 1, 0)
        sens_quantise(1, 0)
        y_product(1, 0, 0, 0)
        y_product(1, 1, 0, 1)
        sens_transpose(2, 2, 6)
        sens_transpose(2, 3, 7)
        y_square(1, 0, 0)
        y_square(1, 1, 0)
        sens_copy(2, 2, "scalar")
        sens_copy(2, 3, "scalar")
        shocks_quantise(0, 1)
        v_clip(0, 2, 0)
        v_clip(0, 3, 0)
        sens_quantise(1, 1)
        y_product(1, 2, 0, 2)
        y_product(1, 3, 0, 3)
        sens_transpose(3, 0, 4)
        sens_transpose(3, 1, 5)
        y_square(1, 2, 0)
        y_square(1, 3, 0)
        sens_copy(3, 0, "scalar")
        sens_copy(3, 1, "scalar")
        v_interleave(0, 0, "vector")
        sens_quantise(2, 0)
        y_product(2, 0, 0, 0)
        y_product(2, 1, 0, 1)
        y_square(2, 0, 0)
        y_square(2, 1, 0)
        v_quantise(0, 0)
        v_clip(1, 0, 0)
        sens_quantise(2, 1)
        y_product(2, 2, 0, 2)
        y_product(2, 3, 0, 3)
        sens_transpose(3, 2, 6)
        sens_transpose(3, 3, 7)
        short_turn(2, 0, 2, 4)
        short_turn(2, 2, 4, 5)
        y_square(2, 2, 0)
        y_square(2, 3, 0)
        sens_copy(3, 2, "scalar")
        sens_copy(3, 3, "scalar")
        short_cast(3, "scalar")
        shocks_interleave(1, 1, "vector")
        v_clip(1, 1, 0)
        v_clip(1, 2, 0)
        v_clip(1, 3, 0)
        shocks_quantise(1, 1)
        sens_quantise(3, 0)
        y_product(3, 0, 0, 0)
        y_product(3, 1, 0, 1)
        y_square(3, 0, 0)
        y_square(3, 1, 0)
        v_interleave(1, 0, "vector")
        v_clip(2, 0, 0)
        sens_quantise(3, 1)
        y_product(3, 2, 0, 2)
        y_product(3, 3, 0, 3)
        y_product(0, 0, 1, 6)
        y_product(0, 1, 1, 7)
        y_product(0, 2, 1, 0)
        y_product(0, 3, 1, 1)
        y_square(3, 2, 0)
        y_product(1, 0, 1, 2)
        y_square(3, 3, 0)
        y_product(1, 1, 1, 3)
        y_square(0, 0, 1)
        v_clip(2, 1, 0)
        y_square(0, 1, 1)
        v_clip(2, 2, 0)
        y_square(0, 2, 1)
        v_clip(2, 3, 0)
        v_interleave(2, 0, "gpsimd", 0, POOL_SHARE)
        y_square(0, 3, 1)
        v_quantise(1, 0)
        short_scale_out(2, 0, 2)
        short_turn(3, 0, 2, 4)
        short_scale_out(2, 2, 4)
        short_turn(3, 2, 4, 5)
        y_product(1, 2, 1, 6)
        y_product(1, 3, 1, 7)
        loss_product(0, 0, HALF, 0, 0, 2)
        loss_product(1, 0, HALF, 1, 0, 2)
        v_clip(3, 0, 0)
        y_square(1, 0, 1)
        v_clip(3, 1, 0)
        y_square(1, 1, 1)
        v_interleave(2, 0, "scalar", POOL_SHARE, HALF)
        v_clip(3, 2, 0)
        v_clip(3, 3, 0)
        v_interleave(3, 0, "gpsimd", 0, POOL_SHARE)
        v_interleave(3, 0, "scalar", POOL_SHARE, HALF)
        short_cast(4, "scalar")
        y_square(1, 2, 1)
        y_square(1, 3, 1)
        short_order(4, "scalar")
        short_quantise(2)
        short_scale_out(3, 0, 2)
        loss_product(2, 0, HALF, 4, 0, 2)
        short_scale_out(3, 2, 4)
        short_quantise(3, 0, 2)
        loss_product(3, 0, HALF, 5, 0, 2)
        y_product(2, 0, 1, 2)
        y_product(2, 1, 1, 3)
        y_product(2, 2, 1, 6)
        y_product(2, 3, 1, 7)
        v_quantise(2, 0)
        short_quantise(3, 2, 4)
        v_clip(0, 0, 1)
        y_square(2, 0, 1)
        v_clip(0, 1, 1)
        y_square(2, 1, 1)
        v_clip(0, 2, 1)
        y_square(2, 2, 1)
        v_clip(0, 3, 1)
        y_square(2, 3, 1)
        short_cast(5, "scalar")
        v_clip(1, 0, 1)
        v_clip(1, 1, 1)
        v_quantise(3, 0)
        loss_product(0, 0, HALF, 0, 2, 4)
        loss_product(1, 0, HALF, 1, 2, 4)
        loss_product(2, 0, HALF, 4, 2, 4)
        loss_product(3, 0, HALF, 5, 2, 4)
        y_product(3, 0, 1, 2)
        y_product(3, 1, 1, 3)
        y_product(3, 2, 1, 6)
        y_product(3, 3, 1, 7)
        loss_out(0, 0, HALF, "scalar")
        short_turn_words(4, 0, 2, 0)
        loss_out(1, 0, HALF, "scalar")
        short_turn_words(4, 2, 4, 1)
        loss_out(2, 0, HALF, "scalar")
        loss_out(3, 0, HALF, "scalar")
        y_square(3, 0, 1)
        y_square(3, 1, 1)
        v_clip(1, 2, 1)
        y_square(3, 2, 1)
        v_clip(1, 3, 1)
        y_square(3, 3, 1)
        short_cast(6, "scalar")
        short_order(6, "scalar")
        v_interleave(0, 1, "vector")
        v_clip(2, 0, 1)
        v_clip(2, 1, 1)
        v_quantise(0, 1)
        loss_product(0, 512, HALF, 4, 0, 1)
        loss_product(1, 512, HALF, 5, 0, 1)
        short_turn_words(5, 0, 2, 2)
        short_turn_words(5, 2, 4, 3)
        v_interleave(1, 1, "vector")
        v_clip(2, 2, 1)
        v_clip(2, 3, 1)
        v_interleave(2, 1, "gpsimd", 0, POOL_SHARE)
        v_quantise(1, 1)
        loss_product(0, 512, HALF, 4, 1, 2)
        loss_product(1, 512, HALF, 5, 1, 2)
        loss_product(2, 512, HALF, 6, 0, 2)
        loss_product(3, 512, HALF, 7, 0, 2)
        short_scale_out(4, 0, 2)
        short_scale_out(4, 2, 4)
        short_quantise(4, 0, 2)
        v_interleave(2, 1, "vector", POOL_SHARE, HALF)
        short_quantise(4, 2, 4)
        loss_product(4, 0, HALF, 0, 0, 4)
        loss_product(4, 512, HALF, 1, 0, 2)
        loss_out(4, 0, HALF, "scalar")
        v_clip(3, 0, 1)
        v_clip(3, 1, 1)
        v_clip(3, 2, 1)
        v_clip(3, 3, 1)
        v_interleave(3, 1, "gpsimd", 0, POOL_SHARE)
        v_interleave(3, 1, "scalar", POOL_SHARE, HALF)
        short_cast(7, "scalar")
        short_order(7, "scalar")
        v_quantise(2, 1)
        loss_product(0, 512, HALF, 4, 2, 3)
        loss_product(1, 512, HALF, 5, 2, 3)
        loss_product(2, 512, HALF, 6, 2, 3)
        loss_product(3, 512, HALF, 7, 2, 3)
        loss_product(4, 512, HALF, 1, 2, 3)
        short_turn_words(6, 0, 2, 0)
        short_scale_out(5, 0, 2)
        short_turn_words(6, 2, 4, 2)
        short_scale_out(5, 2, 4)
        short_quantise(5, 0, 2)
        short_quantise(5, 2, 4)
        loss_product(5, 0, HALF, 3, 0, 4)
        loss_out(5, 0, HALF, "scalar")
        v_quantise(3, 1)
        loss_product(0, 512, HALF, 4, 3, 4)
        loss_product(1, 512, HALF, 5, 3, 4)
        loss_product(2, 512, HALF, 6, 3, 4)
        loss_product(3, 512, HALF, 7, 3, 4)
        loss_product(4, 512, HALF, 1, 3, 4)
        short_turn_words(7, 0, 2, 3)
        loss_out(0, 512, HALF, "scalar")
        short_turn_words(7, 2, 4, 4)
        loss_out(1, 512, HALF, "scalar")
        loss_product(5, 512, HALF, 5, 0, 4)
        loss_out(2, 512, HALF, "scalar")
        loss_out(3, 512, HALF, "scalar")
        loss_out(4, 512, HALF, "scalar")
        loss_out(5, 512, HALF, "scalar")
        short_scale_out(6, 0, 2)
        short_scale_out(6, 2, 4)
        short_quantise(6, 0, 2)
        short_quantise(6, 2, 4)
        loss_product(6, 0, HALF, 6, 0, 4)
        loss_product(6, 512, HALF, 7, 0, 4)
        loss_out(6, 0, HALF, "scalar")
        loss_out(6, 512, HALF, "scalar")
        short_scale_out(7, 0, 2)
        short_scale_out(7, 2, 4)
        short_quantise(7, 0, 2)
        short_quantise(7, 2, 4)
        loss_product(7, 0, HALF, 1, 0, 4)
        loss_product(7, 512, 256, 0)
        loss_product(7, 768, 256, 2)
        loss_out(7, 0, HALF, "scalar")
        loss_out(7, 512, 256, "vector")
        loss_out(7, 768, 256, "scalar")
